import numpy as np
import ml_dtypes


def mxq(x, axis, fmt="e4m3"):
    dtype, down = {"e4m3": (ml_dtypes.float8_e4m3fn, 7), "e5m2": (ml_dtypes.float8_e5m2, 14)}[fmt]
    v = np.moveaxis(np.asarray(x, np.float32).astype(ml_dtypes.bfloat16).astype(np.float64), axis, -1)
    blocks = v.reshape(v.shape[:-1] + (-1, 32))
    amax = np.abs(blocks).max(-1, keepdims=True)
    byte = np.maximum(np.where(amax > 0, np.frexp(amax)[1] - 1 + 127, 0) - down, 1)
    scale = np.exp2(byte - 127.0)
    codes = (blocks / scale).astype(np.float32).astype(dtype).astype(np.float64)
    return np.moveaxis((codes * scale).reshape(v.shape), -1, axis)


WIDE = False


def mx_kscale(k):
    if not WIDE:
        return np.ones(k)
    levels = np.array([10, -10, 5, -5, 0])
    if k % 512:
        return np.exp2(np.random.permutation(np.resize(levels, k // 32))).repeat(32)
    a = np.empty((k // 512, 16))
    for p in range(k // 512):
        a[p, :8] = np.random.permutation(np.resize(levels, 8))
        for g in range(8):
            far = levels[np.abs(levels - a[p, g]) >= 10]
            a[p, g + 8] = far[np.random.randint(len(far))]
    return np.exp2(a.ravel()).repeat(32)


def f64(x):
    return np.asarray(x).astype(np.float64)


def striped(idx):
    return np.tile(idx.reshape(-1, 16).T, (8, 1)).astype(np.uint16)


def unstriped(offs):
    return offs[:16].T.reshape(-1).astype(np.int64)


def pack_weight(w):
    k, n = w.shape
    w = f64(np.asarray(w, np.float32).astype(ml_dtypes.bfloat16)).reshape(k // 32, 32, n)
    amax = np.abs(w).max(1)
    byte = np.clip(np.where(amax > 0, np.frexp(amax)[1] - 1 + 127 - 7, 1), 1, 254)
    scaled = (w * np.exp2(127.0 - byte)[:, None, :]).reshape(k, n).astype(np.float32)
    words = np.ascontiguousarray(scaled.reshape(k // 512, 128, 4, n).transpose(0, 1, 3, 2)).astype(ml_dtypes.float8_e4m3fn).view(np.uint8)
    return words, np.ascontiguousarray(byte.astype(np.uint8).reshape(k // 512, 16, n))


def unpack_weight(words, scales):
    g, p, n, _ = words.shape
    vals = np.ascontiguousarray(words).view(ml_dtypes.float8_e4m3fn).astype(np.float64) * np.repeat(np.exp2(scales.astype(np.float64) - 127.0), 8, axis=1)[..., None]
    return vals.transpose(0, 1, 3, 2).reshape(g * 512, n)


def planes(y):
    n, m = y.shape
    v = y.astype(np.float32).astype(ml_dtypes.bfloat16).astype(np.float64).reshape(n // 32, 32, m)
    top = np.abs(v).max(1)
    byte = np.clip(np.where(top > 0, np.frexp(top)[1] - 1 + 127 - 7, 1), 1, 254)
    codes = (v * np.exp2(127.0 - byte)[:, None, :]).reshape(n, m).astype(np.float32).astype(ml_dtypes.float8_e4m3fn).view(np.uint8)
    words = codes.reshape(n // 512, 128, 4, m).transpose(0, 1, 3, 2)
    return np.ascontiguousarray(words), np.ascontiguousarray(byte.astype(np.uint8).reshape(n // 512, 16, m))


K, T, S, H, N = 1024, 2048, 512, 512, 512
P = 2 ** 7


def setup_inputs():
    n = np.random.standard_normal
    s = mx_kscale(K)[:, None]
    u = mx_kscale(H)
    packed_xT = pack_weight(n((K, T)) * s)
    return {
        "x_words": packed_xT[0],
        "x_scales": packed_xT[1],
        "w1": (n((K, H)) / np.sqrt(K) / s * u).astype(np.float32),
        "w2": (n((H, N)) / np.sqrt(H) / u[:, None]).astype(np.float32),
        "own1": (np.tile(n(S) * 0.7, (P, 1))).astype(np.float32),
        "oth1": (np.tile(n(S) * 0.7, (P, 1))).astype(np.float32),
        "own2": (np.tile(n(S) * 0.7, (P, 1))).astype(np.float32),
        "oth2": (np.tile(n(S) * 0.7, (P, 1))).astype(np.float32),
        "offs": striped(np.random.permutation(T)[:S]),
        "mix1": striped(np.random.permutation(S)),
        "mix2": striped(np.random.permutation(S)),
    }


def reference(x_words, x_scales, w1, w2, own1, oth1, own2, oth2, offs, mix1, mix2):
    xq = unpack_weight(x_words, x_scales)[:, unstriped(offs)]
    y = mxq(f64(w1), 0, "e4m3").T @ xq
    h1 = y * f64(own1)[:1] + y[:, unstriped(mix1)] * f64(oth1)[:1]
    h2 = h1 * f64(own2)[:1] + h1[:, unstriped(mix2)] * f64(oth2)[:1]
    out_0 = mxq(f64(w2), 0, "e4m3").T @ mxq(h2, 0, "e4m3")
    return (out_0,) + planes(out_0)

@@ -1,0 +1,205 @@
+from contextlib import ExitStack
+
+import concourse.mybir as mybir
+from concourse.masks import make_identity
+
+K, T, S, H, N = 1024, 2048, 512, 512, 512
+FLOPS = 2 * S * H * (K + N)
+
+F32 = mybir.dt.float32
+BF16 = mybir.dt.bfloat16
+I32 = mybir.dt.int32
+U32 = mybir.dt.uint32
+U16 = mybir.dt.uint16
+U8 = mybir.dt.uint8
+FP8X4 = mybir.dt.float8_e4m3fn_x4
+MULT = mybir.AluOpType.mult
+ADD = mybir.AluOpType.add
+COPY = mybir.ActivationFunctionType.Copy
+
+P = 128
+PACK = 4
+K_PASS = P * PACK
+PASSES = K // K_PASS
+CHUNKS = S // P
+SPARE = 16
+LIST_COLS = P // 16
+V_SHARE = 80
+
+
+def deal_and_round(engine_copy, dealt, raw, lo, hi):
+    engine_copy(
+        out=dealt[:].rearrange("p (t m j) -> p m t j", t=PACK, j=PACK)[:, lo:hi],
+        in_=raw[:].rearrange("p j (m t) -> p m t j", t=PACK)[:, lo:hi],
+    )
+
+
+def tile_picked_ybutter_none_po_kernel(tc, x_words, x_scales, w1, w2, own1, oth1, own2, oth2, offs, mix1, mix2, out_0, out_1, out_2):
+    nc = tc.nc
+    with ExitStack() as ctx:
+        lists = ctx.enter_context(tc.tile_pool(name="lists", bufs=1))
+        keep = ctx.enter_context(tc.tile_pool(name="keep", bufs=1))
+        ring = ctx.enter_context(tc.tile_pool(name="ring", bufs=2))
+        psum = ctx.enter_context(tc.psum_pool(name="psum", bufs=1))
+
+        offs_sb = lists.tile([P, S // 16], U16, name="offs_sb")
+        mix1_sb = lists.tile([P, S // 16], U16, name="mix1_sb")
+        mix2_sb = lists.tile([P, S // 16], U16, name="mix2_sb")
+
+        w1_raw = [keep.tile([P, PACK, H], F32, name="w1_raw%d" % g) for g in range(PASSES)]
+        w2_raw = keep.tile([P, PACK, N], F32, name="w2_raw")
+        x_table = [keep.tile([P, T], I32, name="x_table%d" % g, align_bytes=64) for g in range(PASSES)]
+        xs_table = keep.tile([P, T], U8, name="xs_table", align_bytes=64)
+        oth1_sb = keep.tile([P, S], F32, name="oth1_sb")
+        oth2_sb = keep.tile([P, S], F32, name="oth2_sb")
+        own_rows = keep.tile([P, P], F32, name="own_rows")
+        own_cols = keep.tile([P, 2 * CHUNKS], F32, name="own_cols")
+        ident = keep.tile([P, P], F32, name="ident")
+        y = [keep.tile([P, S + SPARE], F32, name="y%d" % t, align_bytes=64) for t in range(PACK)]
+        h1 = [keep.tile([P, S], F32, name="h1_%d" % t, align_bytes=64) for t in range(PACK)]
+
+        nc.vector.memset(xs_table[:].bitcast(I32), 0)
+        nc.gpsimd.memset(own_rows[:], 0.0)
+        make_identity(nc, ident[:])
+        for t in range(PACK):
+            nc.gpsimd.memset(y[t][:, S:], 0.0)
+
+        for g in range(PASSES):
+            nc.sync.dma_start(out=w1_raw[g][:], in_=w1[g * K_PASS:(g + 1) * K_PASS, :].rearrange("(p j) c -> p j c", j=PACK))
+        nc.sync.dma_start(offs_sb[:], offs)
+        for q in range(4):
+            nc.scalar.dma_start(out=xs_table[32 * q:32 * q + 4 * PASSES, :].bitcast(I32), in_=x_scales[:, 4 * q:4 * q + 4, :].bitcast(I32))
+        for g in range(PASSES):
+            nc.sync.dma_start(out=x_table[g][:], in_=x_words[g].rearrange("p n t -> p (n t)").bitcast(I32))
+        for r, own in enumerate((own1, own2)):
+            nc.scalar.dma_start(out=own_rows[CHUNKS * r:CHUNKS * (r + 1), :], in_=own[0].rearrange("(c p) -> c p", p=P))
+        nc.sync.dma_start(mix1_sb[:], mix1)
+        nc.sync.dma_start(out=oth1_sb[:], in_=oth1)
+        nc.sync.dma_start(out=w2_raw[:], in_=w2.rearrange("(p j) c -> p j c", j=PACK))
+        nc.sync.dma_start(mix2_sb[:], mix2)
+        nc.sync.dma_start(out=oth2_sb[:], in_=oth2)
+
+        w1_codes, w1_scales = [], []
+        for g in range(PASSES):
+            dealt = keep.tile([P, PACK * H], BF16, name="w1_dealt%d" % g, align_bytes=64)
+            deal_and_round(nc.vector.tensor_copy, dealt, w1_raw[g], 0, V_SHARE)
+            deal_and_round(nc.scalar.copy, dealt, w1_raw[g], V_SHARE, P)
+            codes = keep.tile([P, H], U32, name="w1_codes%d" % g, align_bytes=64)
+            scales = keep.tile([P, H], U8, name="w1_scales%d" % g, align_bytes=64)
+            nc.vector.quantize_mx(out=codes[:].bitcast(FP8X4), scales=scales[:], in_=dealt[:])
+            w1_codes.append(codes)
+            w1_scales.append(scales)
+
+        own_bank = psum.tile([P, CHUNKS, P], F32, name="own_bank", tag="turn", bufs=2)
+        nc.tensor.transpose(own_bank[:, 0, :], own_rows[:], ident[:])
+        nc.scalar.activation(own_cols[:], own_bank[:, 0, 0:2 * CHUNKS], COPY)
+
+        xs = keep.tile([P, S], U8, name="xs", align_bytes=64)
+        nc.vector.tensor_copy(xs[:], xs_table[:].indirect(offs_sb[:]))
+        x_codes = []
+        for g in range(PASSES):
+            codes = keep.tile([P, S], U32, name="x_codes%d" % g, align_bytes=64)
+            nc.vector.tensor_copy(codes[:], x_table[g][:].bitcast(U32).indirect(offs_sb[:]))
+            x_codes.append(codes)
+
+        y_banks = [psum.tile([P, S], F32, name="y_bank%d" % t, tag="wide", bufs=4) for t in range(PACK)]
+        for g in range(PASSES):
+            for t in range(PACK):
+                cols = slice(t * P, (t + 1) * P)
+                nc.tensor.matmul_mx(
+                    out=y_banks[t][:], lhsT=w1_codes[g][:, cols].bitcast(FP8X4), lhsT_scale=w1_scales[g][:, cols],
+                    rhs=x_codes[g][:].bitcast(FP8X4), rhs_scale=xs[4 * g:, :], start=(g == 0), stop=(g == PASSES - 1))
+
+        partner = []
+        own_part = []
+        for t in range(PACK):
+            nc.scalar.copy(out=y[t][:, :S], in_=y_banks[t][:])
+        for t in range(PACK):
+            gathered = keep.tile([P, S], F32, name="partner1_%d" % t)
+            nc.vector.tensor_tensor(gathered[:], y[t][:].indirect(mix1_sb[:]), oth1_sb[:], MULT)
+            partner.append(gathered)
+            turned = psum.tile([P, CHUNKS, P], F32, name="y_turned%d" % t, tag="turn", bufs=2)
+            for c in range(CHUNKS):
+                nc.tensor.transpose(turned[:, c, :], y[t][:, c * P:(c + 1) * P], ident[:])
+            scaled = ring.tile([P, CHUNKS, P], F32, name="scaled1")
+            for c in range(CHUNKS):
+                nc.scalar.activation(scaled[:, c, :], turned[:, c, :], COPY, scale=own_cols[:, c:c + 1])
+            back = psum.tile([P, CHUNKS, P], F32, name="own1_back%d" % t, tag="back", bufs=2)
+            for c in range(CHUNKS):
+                nc.tensor.transpose(back[:, c, :], scaled[:, c, :], ident[:])
+            own_part.append(back)
+            if t > 0:
+                nc.vector.tensor_tensor(h1[t - 1][:], own_part[t - 1][:].rearrange("p c n -> p (c n)"), partner[t - 1][:], ADD)
+        nc.vector.tensor_tensor(h1[PACK - 1][:], own_part[PACK - 1][:].rearrange("p c n -> p (c n)"), partner[PACK - 1][:], ADD)
+
+        w2_dealt = keep.tile([P, PACK * N], BF16, name="w2_dealt", align_bytes=64)
+        deal_and_round(nc.scalar.copy, w2_dealt, w2_raw, 0, P)
+        w2_codes = keep.tile([P, N], U32, name="w2_codes", align_bytes=64)
+        w2_scales = keep.tile([P, N], U8, name="w2_scales", align_bytes=64)
+        nc.vector.quantize_mx(out=w2_codes[:].bitcast(FP8X4), scales=w2_scales[:], in_=w2_dealt[:])
+
+        h1_turned = [psum.tile([P, PACK, P], F32, name="h1_turned%d" % c, tag="wide", bufs=4) for c in range(CHUNKS)]
+        for t in range(PACK):
+            for c in range(CHUNKS):
+                nc.tensor.transpose(h1_turned[c][:, t, :], h1[t][:, c * P:(c + 1) * P], ident[:])
+
+        out_words = keep.tile([P, S], U32, name="out_words", align_bytes=64)
+        out_scales = keep.tile([P, S], U8, name="out_scales", align_bytes=64)
+        out_rows = out_0.rearrange("(p t) n -> p t n", t=PACK)
+        words_hbm = out_1[0].rearrange("p n t -> p (n t)").bitcast(I32)
+        partner2, own2_part, h2_codes, h2_scales, results = {}, {}, {}, {}, {}
+
+        def gather2(c):
+            gathered = ring.tile([P, PACK, P], F32, name="partner2")
+            for t in range(PACK):
+                nc.vector.tensor_tensor(gathered[:, t, :], h1[t][:].indirect(mix2_sb[:, c * LIST_COLS:(c + 1) * LIST_COLS]),
+                                        oth2_sb[:, c * P:(c + 1) * P], MULT)
+            partner2[c] = gathered
+            scaled = ring.tile([P, PACK, P], F32, name="scaled2")
+            nc.scalar.activation(scaled[:], h1_turned[c][:], COPY, scale=own_cols[:, CHUNKS + c:CHUNKS + c + 1])
+            back = psum.tile([P, PACK, P], F32, name="own2_back%d" % c, tag="back", bufs=2)
+            for t in range(PACK):
+                nc.tensor.transpose(back[:, t, :], scaled[:, t, :], ident[:])
+            own2_part[c] = back
+
+        def add2(c):
+            h2 = ring.tile([P, P, PACK], BF16, name="h2", align_bytes=64)
+            nc.vector.tensor_tensor(h2[:], own2_part[c][:].rearrange("p t n -> p n t"), partner2[c][:].rearrange("p t n -> p n t"), ADD)
+            h2_codes[c] = h2
+
+        def product2(c):
+            h2 = h2_codes[c]
+            codes = ring.tile([P, P], U32, name="h2_codes", align_bytes=64)
+            scales = ring.tile([P, P], U8, name="h2_scales", align_bytes=64)
+            nc.vector.quantize_mx(out=codes[:].bitcast(FP8X4), scales=scales[:], in_=h2[:].rearrange("p n t -> p (n t)"))
+            bank = psum.tile([P, PACK, P], F32, name="out_bank%d" % c, tag="turn", bufs=2)
+            for t in range(PACK):
+                cols = slice(t * P, (t + 1) * P)
+                nc.tensor.matmul_mx(out=bank[:, t, :], lhsT=w2_codes[:, cols].bitcast(FP8X4), lhsT_scale=w2_scales[:, cols],
+                                    rhs=codes[:].bitcast(FP8X4), rhs_scale=scales[:], start=True, stop=True)
+            rounded = ring.tile([P, P, PACK], BF16, name="rounded", align_bytes=64)
+            copy_rounded = nc.vector.tensor_copy if c == CHUNKS - 1 else nc.scalar.copy
+            copy_rounded(out=rounded[:], in_=bank[:].rearrange("p t n -> p n t"))
+            result = keep.tile([P, PACK, P], F32, name="result%d" % c)
+            nc.scalar.copy(out=result[:], in_=bank[:])
+            nc.sync.dma_start(out=out_rows[:, :, c * P:(c + 1) * P], in_=result[:])
+            results[c] = rounded
+
+        def planes(c):
+            cols = slice(c * P, (c + 1) * P)
+            nc.vector.quantize_mx(out=out_words[:, cols].bitcast(FP8X4), scales=out_scales[:, cols],
+                                  in_=results[c][:].rearrange("p n t -> p (n t)"))
+            nc.sync.dma_start(out=words_hbm[:, cols], in_=out_words[:, cols].bitcast(I32))
+
+        for step in range(CHUNKS + 3):
+            if step < CHUNKS:
+                gather2(step)
+            if 0 <= step - 2 < CHUNKS:
+                product2(step - 2)
+            if 0 <= step - 1 < CHUNKS:
+                add2(step - 1)
+            if 0 <= step - 3 < CHUNKS:
+                planes(step - 3)
+        for q in range(4):
+            queue = nc.sync if q % 2 == 0 else nc.scalar
+            queue.dma_start(out=out_2[0, 4 * q:4 * q + 4, :].bitcast(I32), in_=out_scales[32 * q:32 * q + 4, :].bitcast(I32))

@@ -58,22 +58,28 @@ def tile_picked_ybutter_none_po_kernel(tc, x_words, x_scales, w1, w2, own1, oth1
         y = [keep.tile([P, S + SPARE], F32, name="y%d" % t, align_bytes=64) for t in range(PACK)]
         h1 = [keep.tile([P, S], F32, name="h1_%d" % t, align_bytes=64) for t in range(PACK)]
 
-        nc.vector.memset(xs_table[:].bitcast(I32), 0)
+        nc.gpsimd.memset(xs_table[:].bitcast(I32), 0)
         nc.gpsimd.memset(own_rows[:], 0.0)
         make_identity(nc, ident[:])
         for t in range(PACK):
             nc.gpsimd.memset(y[t][:, S:], 0.0)
 
-        for g in range(PASSES):
+        def load_w1(g):
             nc.sync.dma_start(out=w1_raw[g][:], in_=w1[g * K_PASS:(g + 1) * K_PASS, :].rearrange("(p j) c -> p j c", j=PACK))
-        nc.sync.dma_start(offs_sb[:], offs)
-        for q in range(4):
-            nc.scalar.dma_start(out=xs_table[32 * q:32 * q + 4 * PASSES, :].bitcast(I32), in_=x_scales[:, 4 * q:4 * q + 4, :].bitcast(I32))
-        for g in range(PASSES):
+
+        def load_x(g):
             nc.sync.dma_start(out=x_table[g][:], in_=x_words[g].rearrange("p n t -> p (n t)").bitcast(I32))
-        for r, own in enumerate((own1, own2)):
-            nc.scalar.dma_start(out=own_rows[CHUNKS * r:CHUNKS * (r + 1), :], in_=own[0].rearrange("(c p) -> c p", p=P))
+
+        load_w1(0)
+        nc.sync.dma_start(offs_sb[:], offs)
+        load_x(0)
         nc.sync.dma_start(mix1_sb[:], mix1)
+        for q in range(4):
+            nc.sync.dma_start(out=xs_table[32 * q:32 * q + 4 * PASSES, :].bitcast(I32), in_=x_scales[:, 4 * q:4 * q + 4, :].bitcast(I32))
+        load_w1(1)
+        for r, own in enumerate((own1, own2)):
+            nc.sync.dma_start(out=own_rows[CHUNKS * r:CHUNKS * (r + 1), :], in_=own[0].rearrange("(c p) -> c p", p=P))
+        load_x(1)
         nc.sync.dma_start(out=oth1_sb[:], in_=oth1)
         nc.sync.dma_start(out=w2_raw[:], in_=w2.rearrange("(p j) c -> p j c", j=PACK))
         nc.sync.dma_start(mix2_sb[:], mix2)
@@ -90,7 +96,7 @@ def tile_picked_ybutter_none_po_kernel(tc, x_words, x_scales, w1, w2, own1, oth1
             w1_codes.append(codes)
             w1_scales.append(scales)
 
-        own_bank = psum.tile([P, CHUNKS, P], F32, name="own_bank", tag="turn", bufs=2)
+        own_bank = psum.tile([P, CHUNKS, P], F32, name="own_bank", tag="bank7")
         nc.tensor.transpose(own_bank[:, 0, :], own_rows[:], ident[:])
         nc.scalar.activation(own_cols[:], own_bank[:, 0, 0:2 * CHUNKS], COPY)
 
@@ -102,7 +108,7 @@ def tile_picked_ybutter_none_po_kernel(tc, x_words, x_scales, w1, w2, own1, oth1
             nc.vector.tensor_copy(codes[:], x_table[g][:].bitcast(U32).indirect(offs_sb[:]))
             x_codes.append(codes)
 
-        y_banks = [psum.tile([P, S], F32, name="y_bank%d" % t, tag="wide", bufs=4) for t in range(PACK)]
+        y_banks = [psum.tile([P, S], F32, name="y_bank%d" % t, tag="bank%d" % t) for t in range(PACK)]
         for g in range(PASSES):
             for t in range(PACK):
                 cols = slice(t * P, (t + 1) * P)
@@ -118,13 +124,13 @@ def tile_picked_ybutter_none_po_kernel(tc, x_words, x_scales, w1, w2, own1, oth1
             gathered = keep.tile([P, S], F32, name="partner1_%d" % t)
             nc.vector.tensor_tensor(gathered[:], y[t][:].indirect(mix1_sb[:]), oth1_sb[:], MULT)
             partner.append(gathered)
-            turned = psum.tile([P, CHUNKS, P], F32, name="y_turned%d" % t, tag="turn", bufs=2)
+            turned = psum.tile([P, CHUNKS, P], F32, name="y_turned%d" % t, tag="bank%d" % (4 + t % 2))
             for c in range(CHUNKS):
                 nc.tensor.transpose(turned[:, c, :], y[t][:, c * P:(c + 1) * P], ident[:])
-            scaled = ring.tile([P, CHUNKS, P], F32, name="scaled1")
+            scaled = keep.tile([P, CHUNKS, P], F32, name="scaled1_%d" % t, tag="scaled1_%d" % t, align_bytes=64)
             for c in range(CHUNKS):
                 nc.scalar.activation(scaled[:, c, :], turned[:, c, :], COPY, scale=own_cols[:, c:c + 1])
-            back = psum.tile([P, CHUNKS, P], F32, name="own1_back%d" % t, tag="back", bufs=2)
+            back = psum.tile([P, CHUNKS, P], F32, name="own1_back%d" % t, tag="bank%d" % ((6 + t) % 8))
             for c in range(CHUNKS):
                 nc.tensor.transpose(back[:, c, :], scaled[:, c, :], ident[:])
             own_part.append(back)
@@ -132,13 +138,13 @@ def tile_picked_ybutter_none_po_kernel(tc, x_words, x_scales, w1, w2, own1, oth1
                 nc.vector.tensor_tensor(h1[t - 1][:], own_part[t - 1][:].rearrange("p c n -> p (c n)"), partner[t - 1][:], ADD)
         nc.vector.tensor_tensor(h1[PACK - 1][:], own_part[PACK - 1][:].rearrange("p c n -> p (c n)"), partner[PACK - 1][:], ADD)
 
-        w2_dealt = keep.tile([P, PACK * N], BF16, name="w2_dealt", align_bytes=64)
+        w2_dealt = keep.tile([P, PACK * N], BF16, name="w2_dealt", tag="scaled1_2", align_bytes=64)
         deal_and_round(nc.scalar.copy, w2_dealt, w2_raw, 0, P)
         w2_codes = keep.tile([P, N], U32, name="w2_codes", align_bytes=64)
         w2_scales = keep.tile([P, N], U8, name="w2_scales", align_bytes=64)
         nc.vector.quantize_mx(out=w2_codes[:].bitcast(FP8X4), scales=w2_scales[:], in_=w2_dealt[:])
 
-        h1_turned = [psum.tile([P, PACK, P], F32, name="h1_turned%d" % c, tag="wide", bufs=4) for c in range(CHUNKS)]
+        h1_turned = [psum.tile([P, PACK, P], F32, name="h1_turned%d" % c, tag="bank%d" % (2 + c)) for c in range(CHUNKS)]
         for t in range(PACK):
             for c in range(CHUNKS):
                 nc.tensor.transpose(h1_turned[c][:, t, :], h1[t][:, c * P:(c + 1) * P], ident[:])
@@ -150,14 +156,14 @@ def tile_picked_ybutter_none_po_kernel(tc, x_words, x_scales, w1, w2, own1, oth1
         partner2, own2_part, h2_codes, h2_scales, results = {}, {}, {}, {}, {}
 
         def gather2(c):
-            gathered = ring.tile([P, PACK, P], F32, name="partner2")
+            gathered = keep.tile([P, PACK, P], F32, name="partner2_%d" % c, tag="partner2_%d" % min(c, 1))
             for t in range(PACK):
                 nc.vector.tensor_tensor(gathered[:, t, :], h1[t][:].indirect(mix2_sb[:, c * LIST_COLS:(c + 1) * LIST_COLS]),
                                         oth2_sb[:, c * P:(c + 1) * P], MULT)
             partner2[c] = gathered
-            scaled = ring.tile([P, PACK, P], F32, name="scaled2")
+            scaled = keep.tile([P, PACK, P], F32, name="scaled2_%d" % c)
             nc.scalar.activation(scaled[:], h1_turned[c][:], COPY, scale=own_cols[:, CHUNKS + c:CHUNKS + c + 1])
-            back = psum.tile([P, PACK, P], F32, name="own2_back%d" % c, tag="back", bufs=2)
+            back = psum.tile([P, PACK, P], F32, name="own2_back%d" % c, tag="bank%d" % ((6 + c) % 8))
             for t in range(PACK):
                 nc.tensor.transpose(back[:, t, :], scaled[:, t, :], ident[:])
             own2_part[c] = back
@@ -172,7 +178,7 @@ def tile_picked_ybutter_none_po_kernel(tc, x_words, x_scales, w1, w2, own1, oth1
             codes = ring.tile([P, P], U32, name="h2_codes", align_bytes=64)
             scales = ring.tile([P, P], U8, name="h2_scales", align_bytes=64)
             nc.vector.quantize_mx(out=codes[:].bitcast(FP8X4), scales=scales[:], in_=h2[:].rearrange("p n t -> p (n t)"))
-            bank = psum.tile([P, PACK, P], F32, name="out_bank%d" % c, tag="turn", bufs=2)
+            bank = psum.tile([P, PACK, P], F32, name="out_bank%d" % c, tag="bank%d" % (2 + c))
             for t in range(PACK):
                 cols = slice(t * P, (t + 1) * P)
                 nc.tensor.matmul_mx(out=bank[:, t, :], lhsT=w2_codes[:, cols].bitcast(FP8X4), lhsT_scale=w2_scales[:, cols],
@@ -191,15 +197,19 @@ def tile_picked_ybutter_none_po_kernel(tc, x_words, x_scales, w1, w2, own1, oth1
                                   in_=results[c][:].rearrange("p n t -> p (n t)"))
             nc.sync.dma_start(out=words_hbm[:, cols], in_=out_words[:, cols].bitcast(I32))
 
-        for step in range(CHUNKS + 3):
-            if step < CHUNKS:
-                gather2(step)
-            if 0 <= step - 2 < CHUNKS:
-                product2(step - 2)
-            if 0 <= step - 1 < CHUNKS:
-                add2(step - 1)
-            if 0 <= step - 3 < CHUNKS:
-                planes(step - 3)
+        gather2(0)
+        gather2(1)
+        add2(0)
+        for c in range(1, CHUNKS):
+            add2(c)
+            product2(c - 1)
+            if c > 1:
+                planes(c - 2)
+            if c + 1 < CHUNKS:
+                gather2(c + 1)
+        product2(CHUNKS - 1)
+        planes(CHUNKS - 2)
+        planes(CHUNKS - 1)
         for q in range(4):
             queue = nc.sync if q % 2 == 0 else nc.scalar
             queue.dma_start(out=out_2[0, 4 * q:4 * q + 4, :].bitcast(I32), in_=out_scales[32 * q:32 * q + 4, :].bitcast(I32))

@@ -23,8 +23,9 @@ K_PASS = P * PACK
 PASSES = K // K_PASS
 CHUNKS = S // P
 SPARE = 16
-LIST_COLS = P // 16
 V_SHARE = 80
+DIRECT = 2
+PIECES = [(0, 128), (128, 128), (256, 128), (384, 128)]
 
 
 def deal_and_round(engine_copy, dealt, raw, lo, hi):
@@ -50,13 +51,13 @@ def tile_picked_ybutter_none_po_kernel(tc, x_words, x_scales, w1, w2, own1, oth1
         w2_raw = keep.tile([P, PACK, N], F32, name="w2_raw")
         x_table = [keep.tile([P, T], I32, name="x_table%d" % g, align_bytes=64) for g in range(PASSES)]
         xs_table = keep.tile([P, T], U8, name="xs_table", align_bytes=64)
+        own1_sb = keep.tile([P, S], F32, name="own1_sb")
         oth1_sb = keep.tile([P, S], F32, name="oth1_sb")
         oth2_sb = keep.tile([P, S], F32, name="oth2_sb")
         own_rows = keep.tile([P, P], F32, name="own_rows")
         own_cols = keep.tile([P, 2 * CHUNKS], F32, name="own_cols")
         ident = keep.tile([P, P], F32, name="ident")
         y = [keep.tile([P, S + SPARE], F32, name="y%d" % t, align_bytes=64) for t in range(PACK)]
-        h1 = [keep.tile([P, S], F32, name="h1_%d" % t, align_bytes=64) for t in range(PACK)]
 
         nc.gpsimd.memset(xs_table[:].bitcast(I32), 0)
         nc.gpsimd.memset(own_rows[:], 0.0)
@@ -80,6 +81,7 @@ def tile_picked_ybutter_none_po_kernel(tc, x_words, x_scales, w1, w2, own1, oth1
         for r, own in enumerate((own1, own2)):
             nc.sync.dma_start(out=own_rows[CHUNKS * r:CHUNKS * (r + 1), :], in_=own[0].rearrange("(c p) -> c p", p=P))
         load_x(1)
+        nc.sync.dma_start(out=own1_sb[:], in_=own1)
         nc.sync.dma_start(out=oth1_sb[:], in_=oth1)
         nc.sync.dma_start(out=w2_raw[:], in_=w2.rearrange("(p j) c -> p j c", j=PACK))
         nc.sync.dma_start(mix2_sb[:], mix2)
@@ -96,7 +98,7 @@ def tile_picked_ybutter_none_po_kernel(tc, x_words, x_scales, w1, w2, own1, oth1
             w1_codes.append(codes)
             w1_scales.append(scales)
 
-        own_bank = psum.tile([P, CHUNKS, P], F32, name="own_bank", tag="bank7")
+        own_bank = psum.tile([P, CHUNKS, P], F32, name="own_bank", tag="bank4")
         nc.tensor.transpose(own_bank[:, 0, :], own_rows[:], ident[:])
         nc.scalar.activation(own_cols[:], own_bank[:, 0, 0:2 * CHUNKS], COPY)
 
@@ -105,38 +107,50 @@ def tile_picked_ybutter_none_po_kernel(tc, x_words, x_scales, w1, w2, own1, oth1
         x_codes = []
         for g in range(PASSES):
             codes = keep.tile([P, S], U32, name="x_codes%d" % g, align_bytes=64)
-            nc.vector.tensor_copy(codes[:], x_table[g][:].bitcast(U32).indirect(offs_sb[:]))
+            pieces = 2 if g == PASSES - 1 else 1
+            for h in range(pieces):
+                lo, hi = h * S // pieces, (h + 1) * S // pieces
+                nc.vector.tensor_copy(codes[:, lo:hi], x_table[g][:].bitcast(U32).indirect(offs_sb[:, lo // 16:hi // 16]))
             x_codes.append(codes)
 
         y_banks = [psum.tile([P, S], F32, name="y_bank%d" % t, tag="bank%d" % t) for t in range(PACK)]
+        y0_late = psum.tile([P, S], F32, name="y0_late", tag="bank5")
+        groups = [(0, y_banks[0], slice(0, S // 2)), (0, y0_late, slice(S // 2, S))]
+        groups.extend((t, y_banks[t], slice(0, S)) for t in range(1, PACK))
         for g in range(PASSES):
-            for t in range(PACK):
+            for t, bank, tokens in groups:
                 cols = slice(t * P, (t + 1) * P)
                 nc.tensor.matmul_mx(
-                    out=y_banks[t][:], lhsT=w1_codes[g][:, cols].bitcast(FP8X4), lhsT_scale=w1_scales[g][:, cols],
-                    rhs=x_codes[g][:].bitcast(FP8X4), rhs_scale=xs[4 * g:, :], start=(g == 0), stop=(g == PASSES - 1))
+                    out=bank[:, tokens], lhsT=w1_codes[g][:, cols].bitcast(FP8X4), lhsT_scale=w1_scales[g][:, cols],
+                    rhs=x_codes[g][:, tokens].bitcast(FP8X4), rhs_scale=xs[4 * g:, tokens], start=(g == 0), stop=(g == PASSES - 1))
+        for t, bank, tokens in groups:
+            nc.scalar.copy(out=y[t][:, tokens], in_=bank[:, tokens])
 
-        partner = []
-        own_part = []
+        partner, own_part = [], []
         for t in range(PACK):
-            nc.scalar.copy(out=y[t][:, :S], in_=y_banks[t][:])
-        for t in range(PACK):
-            gathered = keep.tile([P, S], F32, name="partner1_%d" % t)
+            gathered = keep.tile([P, S], F32, name="partner1_%d" % t, tag="partner1_%d" % t)
             nc.vector.tensor_tensor(gathered[:], y[t][:].indirect(mix1_sb[:]), oth1_sb[:], MULT)
             partner.append(gathered)
-            turned = psum.tile([P, CHUNKS, P], F32, name="y_turned%d" % t, tag="bank%d" % (4 + t % 2))
+            if t < DIRECT:
+                product = keep.tile([P, S], F32, name="own1_direct%d" % t)
+                for tokens in [tokens for tile_t, bank, tokens in groups if tile_t == t]:
+                    nc.vector.tensor_tensor(product[:, tokens], y[t][:, tokens], own1_sb[:, tokens], MULT)
+                own_part.append(product[:])
+        rest = PACK - DIRECT
+        y_turned = [psum.tile([P, rest, P], F32, name="y_turned%d" % c, tag="bank%d" % (4 + c)) for c in range(CHUNKS)]
+        for e in range(rest):
             for c in range(CHUNKS):
-                nc.tensor.transpose(turned[:, c, :], y[t][:, c * P:(c + 1) * P], ident[:])
-            scaled = keep.tile([P, CHUNKS, P], F32, name="scaled1_%d" % t, tag="scaled1_%d" % t, align_bytes=64)
-            for c in range(CHUNKS):
-                nc.scalar.activation(scaled[:, c, :], turned[:, c, :], COPY, scale=own_cols[:, c:c + 1])
-            back = psum.tile([P, CHUNKS, P], F32, name="own1_back%d" % t, tag="bank%d" % ((6 + t) % 8))
-            for c in range(CHUNKS):
-                nc.tensor.transpose(back[:, c, :], scaled[:, c, :], ident[:])
-            own_part.append(back)
-            if t > 0:
-                nc.vector.tensor_tensor(h1[t - 1][:], own_part[t - 1][:].rearrange("p c n -> p (c n)"), partner[t - 1][:], ADD)
-        nc.vector.tensor_tensor(h1[PACK - 1][:], own_part[PACK - 1][:].rearrange("p c n -> p (c n)"), partner[PACK - 1][:], ADD)
+                nc.tensor.transpose(y_turned[c][:, e, :], y[DIRECT + e][:, c * P:(c + 1) * P], ident[:])
+        back = [psum.tile([P, S], F32, name="own1_back%d" % e, tag="bank%d" % (DIRECT + e)) for e in range(rest)]
+        for c in range(CHUNKS):
+            scaled = keep.tile([P, rest, P], F32, name="scaled1_%d" % c, tag="scaled1_%d" % c, align_bytes=64)
+            nc.scalar.activation(scaled[:], y_turned[c][:], COPY, scale=own_cols[:, c:c + 1])
+            for e in range(rest):
+                nc.tensor.transpose(back[e][:, c * P:(c + 1) * P], scaled[:, e, :], ident[:])
+        own_part.extend(bank[:] for bank in back)
+        h1 = [keep.tile([P, S], F32, name="h1_%d" % t) for t in range(PACK)]
+        for t in range(PACK):
+            nc.vector.tensor_tensor(h1[t][:], own_part[t], partner[t][:], ADD)
 
         w2_dealt = keep.tile([P, PACK * N], BF16, name="w2_dealt", tag="scaled1_2", align_bytes=64)
         deal_and_round(nc.scalar.copy, w2_dealt, w2_raw, 0, P)
@@ -144,72 +158,79 @@ def tile_picked_ybutter_none_po_kernel(tc, x_words, x_scales, w1, w2, own1, oth1
         w2_scales = keep.tile([P, N], U8, name="w2_scales", align_bytes=64)
         nc.vector.quantize_mx(out=w2_codes[:].bitcast(FP8X4), scales=w2_scales[:], in_=w2_dealt[:])
 
-        h1_turned = [psum.tile([P, PACK, P], F32, name="h1_turned%d" % c, tag="bank%d" % (2 + c)) for c in range(CHUNKS)]
-        for t in range(PACK):
-            for c in range(CHUNKS):
+        h1_turned = [psum.tile([P, PACK, P], F32, name="h1_turned%d" % c, tag="bank%d" % (4 + c)) for c in range(CHUNKS)]
+        own2_part = []
+        for c in range(CHUNKS):
+            for t in range(PACK):
                 nc.tensor.transpose(h1_turned[c][:, t, :], h1[t][:, c * P:(c + 1) * P], ident[:])
+            scaled = keep.tile([P, PACK, P], F32, name="scaled2_%d" % c)
+            nc.scalar.activation(scaled[:], h1_turned[c][:], COPY, scale=own_cols[:, CHUNKS + c:CHUNKS + c + 1])
+            back = psum.tile([P, PACK, P], F32, name="own2_back%d" % c, tag="bank%d" % c)
+            for t in range(PACK):
+                nc.tensor.transpose(back[:, t, :], scaled[:, t, :], ident[:])
+            own2_part.append(back)
 
         out_words = keep.tile([P, S], U32, name="out_words", align_bytes=64)
         out_scales = keep.tile([P, S], U8, name="out_scales", align_bytes=64)
         out_rows = out_0.rearrange("(p t) n -> p t n", t=PACK)
         words_hbm = out_1[0].rearrange("p n t -> p (n t)").bitcast(I32)
-        partner2, own2_part, h2_codes, h2_scales, results = {}, {}, {}, {}, {}
+        partner2, h2_tiles, rounded_tiles = {}, {}, {}
 
-        def gather2(c):
-            gathered = keep.tile([P, PACK, P], F32, name="partner2_%d" % c, tag="partner2_%d" % min(c, 1))
+        def gather2(i):
+            lo, n = PIECES[i]
+            gathered = keep.tile([P, PACK, n], F32, name="partner2_%d" % i, tag="partner1_3" if i == 0 else "scaled1_3", align_bytes=None if i == 0 else 64)
             for t in range(PACK):
-                nc.vector.tensor_tensor(gathered[:, t, :], h1[t][:].indirect(mix2_sb[:, c * LIST_COLS:(c + 1) * LIST_COLS]),
-                                        oth2_sb[:, c * P:(c + 1) * P], MULT)
-            partner2[c] = gathered
-            scaled = keep.tile([P, PACK, P], F32, name="scaled2_%d" % c)
-            nc.scalar.activation(scaled[:], h1_turned[c][:], COPY, scale=own_cols[:, CHUNKS + c:CHUNKS + c + 1])
-            back = psum.tile([P, PACK, P], F32, name="own2_back%d" % c, tag="bank%d" % ((6 + c) % 8))
-            for t in range(PACK):
-                nc.tensor.transpose(back[:, t, :], scaled[:, t, :], ident[:])
-            own2_part[c] = back
+                nc.vector.tensor_tensor(gathered[:, t, :], h1[t][:].indirect(mix2_sb[:, lo // 16:(lo + n) // 16]),
+                                        oth2_sb[:, lo:lo + n], MULT)
+            partner2[i] = gathered
 
-        def add2(c):
-            h2 = ring.tile([P, P, PACK], BF16, name="h2", align_bytes=64)
-            nc.vector.tensor_tensor(h2[:], own2_part[c][:].rearrange("p t n -> p n t"), partner2[c][:].rearrange("p t n -> p n t"), ADD)
-            h2_codes[c] = h2
+        def add2(i):
+            lo, n = PIECES[i]
+            h2 = ring.tile([P, n, PACK], BF16, name="h2", align_bytes=64)
+            own_view = own2_part[lo // P][:, :, lo % P:lo % P + n]
+            nc.vector.tensor_tensor(h2[:], own_view.rearrange("p t n -> p n t"), partner2[i][:].rearrange("p t n -> p n t"), ADD)
+            h2_tiles[i] = h2
 
-        def product2(c):
-            h2 = h2_codes[c]
-            codes = ring.tile([P, P], U32, name="h2_codes", align_bytes=64)
-            scales = ring.tile([P, P], U8, name="h2_scales", align_bytes=64)
-            nc.vector.quantize_mx(out=codes[:].bitcast(FP8X4), scales=scales[:], in_=h2[:].rearrange("p n t -> p (n t)"))
-            bank = psum.tile([P, PACK, P], F32, name="out_bank%d" % c, tag="bank%d" % (2 + c))
+        def product2(i):
+            lo, n = PIECES[i]
+            codes = ring.tile([P, n], U32, name="h2_codes", align_bytes=64)
+            scales = ring.tile([P, n], U8, name="h2_scales", align_bytes=64)
+            nc.vector.quantize_mx(out=codes[:].bitcast(FP8X4), scales=scales[:], in_=h2_tiles[i][:].rearrange("p n t -> p (n t)"))
+            bank = psum.tile([P, PACK, n], F32, name="out_bank%d" % i, tag="bank%d" % (4 + i % CHUNKS))
             for t in range(PACK):
                 cols = slice(t * P, (t + 1) * P)
                 nc.tensor.matmul_mx(out=bank[:, t, :], lhsT=w2_codes[:, cols].bitcast(FP8X4), lhsT_scale=w2_scales[:, cols],
                                     rhs=codes[:].bitcast(FP8X4), rhs_scale=scales[:], start=True, stop=True)
-            rounded = ring.tile([P, P, PACK], BF16, name="rounded", align_bytes=64)
-            copy_rounded = nc.vector.tensor_copy if c == CHUNKS - 1 else nc.scalar.copy
-            copy_rounded(out=rounded[:], in_=bank[:].rearrange("p t n -> p n t"))
-            result = keep.tile([P, PACK, P], F32, name="result%d" % c)
+            rounded = ring.tile([P, n, PACK], BF16, name="rounded", align_bytes=64)
+            result = keep.tile([P, PACK, n], F32, name="result%d" % i)
+            if i < len(PIECES) - 1:
+                nc.scalar.copy(out=rounded[:], in_=bank[:].rearrange("p t n -> p n t"))
             nc.scalar.copy(out=result[:], in_=bank[:])
-            nc.sync.dma_start(out=out_rows[:, :, c * P:(c + 1) * P], in_=result[:])
-            results[c] = rounded
+            nc.sync.dma_start(out=out_rows[:, :, lo:lo + n], in_=result[:])
+            if i == len(PIECES) - 1:
+                nc.vector.tensor_copy(out=rounded[:], in_=result[:].rearrange("p t n -> p n t"))
+            rounded_tiles[i] = rounded
 
-        def planes(c):
-            cols = slice(c * P, (c + 1) * P)
-            nc.vector.quantize_mx(out=out_words[:, cols].bitcast(FP8X4), scales=out_scales[:, cols],
-                                  in_=results[c][:].rearrange("p n t -> p (n t)"))
-            nc.sync.dma_start(out=words_hbm[:, cols], in_=out_words[:, cols].bitcast(I32))
+        def planes(i):
+            lo, n = PIECES[i]
+            nc.vector.quantize_mx(out=out_words[:, lo:lo + n].bitcast(FP8X4), scales=out_scales[:, lo:lo + n],
+                                  in_=rounded_tiles[i][:].rearrange("p n t -> p (n t)"))
+            nc.sync.dma_start(out=words_hbm[:, lo:lo + n], in_=out_words[:, lo:lo + n].bitcast(I32))
 
+        last = len(PIECES) - 1
         gather2(0)
         gather2(1)
         add2(0)
-        for c in range(1, CHUNKS):
-            add2(c)
-            product2(c - 1)
-            if c > 1:
-                planes(c - 2)
-            if c + 1 < CHUNKS:
-                gather2(c + 1)
-        product2(CHUNKS - 1)
-        planes(CHUNKS - 2)
-        planes(CHUNKS - 1)
+        for i in range(1, last + 1):
+            add2(i)
+            product2(i - 1)
+            if i > 1:
+                planes(i - 2)
+            if i < last:
+                gather2(i + 1)
+        product2(last)
+        planes(last - 1)
+        planes(last)
         for q in range(4):
             queue = nc.sync if q % 2 == 0 else nc.scalar
             queue.dma_start(out=out_2[0, 4 * q:4 * q + 4, :].bitcast(I32), in_=out_scales[32 * q:32 * q + 4, :].bitcast(I32))

@@ -22,10 +22,10 @@ PACK = 4
 K_PASS = P * PACK
 PASSES = K // K_PASS
 CHUNKS = S // P
+PAIRS = PACK // 2
 SPARE = 16
 V_SHARE = 80
-DIRECT = 2
-PIECES = [(0, 128), (128, 128), (256, 128), (384, 128)]
+LATE = 2
 
 
 def deal_and_round(engine_copy, dealt, raw, lo, hi):
@@ -51,7 +51,6 @@ def tile_picked_ybutter_none_po_kernel(tc, x_words, x_scales, w1, w2, own1, oth1
         w2_raw = keep.tile([P, PACK, N], F32, name="w2_raw")
         x_table = [keep.tile([P, T], I32, name="x_table%d" % g, align_bytes=64) for g in range(PASSES)]
         xs_table = keep.tile([P, T], U8, name="xs_table", align_bytes=64)
-        own1_sb = keep.tile([P, S], F32, name="own1_sb")
         oth1_sb = keep.tile([P, S], F32, name="oth1_sb")
         oth2_sb = keep.tile([P, S], F32, name="oth2_sb")
         own_rows = keep.tile([P, P], F32, name="own_rows")
@@ -59,7 +58,7 @@ def tile_picked_ybutter_none_po_kernel(tc, x_words, x_scales, w1, w2, own1, oth1
         ident = keep.tile([P, P], F32, name="ident")
         y = [keep.tile([P, S + SPARE], F32, name="y%d" % t, align_bytes=64) for t in range(PACK)]
 
-        nc.gpsimd.memset(xs_table[:].bitcast(I32), 0)
+        nc.vector.memset(xs_table[:].bitcast(I32), 0)
         nc.gpsimd.memset(own_rows[:], 0.0)
         make_identity(nc, ident[:])
         for t in range(PACK):
@@ -71,17 +70,19 @@ def tile_picked_ybutter_none_po_kernel(tc, x_words, x_scales, w1, w2, own1, oth1
         def load_x(g):
             nc.sync.dma_start(out=x_table[g][:], in_=x_words[g].rearrange("p n t -> p (n t)").bitcast(I32))
 
+        def load_scales():
+            for q in range(4):
+                nc.sync.dma_start(out=xs_table[32 * q:32 * q + 4 * PASSES, :].bitcast(I32), in_=x_scales[:, 4 * q:4 * q + 4, :].bitcast(I32))
+
         load_w1(0)
         nc.sync.dma_start(offs_sb[:], offs)
-        load_x(0)
-        nc.sync.dma_start(mix1_sb[:], mix1)
-        for q in range(4):
-            nc.sync.dma_start(out=xs_table[32 * q:32 * q + 4 * PASSES, :].bitcast(I32), in_=x_scales[:, 4 * q:4 * q + 4, :].bitcast(I32))
+        load_scales()
         load_w1(1)
+        load_x(0)
+        load_x(1)
+        nc.sync.dma_start(mix1_sb[:], mix1)
         for r, own in enumerate((own1, own2)):
             nc.sync.dma_start(out=own_rows[CHUNKS * r:CHUNKS * (r + 1), :], in_=own[0].rearrange("(c p) -> c p", p=P))
-        load_x(1)
-        nc.sync.dma_start(out=own1_sb[:], in_=own1)
         nc.sync.dma_start(out=oth1_sb[:], in_=oth1)
         nc.sync.dma_start(out=w2_raw[:], in_=w2.rearrange("(p j) c -> p j c", j=PACK))
         nc.sync.dma_start(mix2_sb[:], mix2)
@@ -98,10 +99,6 @@ def tile_picked_ybutter_none_po_kernel(tc, x_words, x_scales, w1, w2, own1, oth1
             w1_codes.append(codes)
             w1_scales.append(scales)
 
-        own_bank = psum.tile([P, CHUNKS, P], F32, name="own_bank", tag="bank4")
-        nc.tensor.transpose(own_bank[:, 0, :], own_rows[:], ident[:])
-        nc.scalar.activation(own_cols[:], own_bank[:, 0, 0:2 * CHUNKS], COPY)
-
         xs = keep.tile([P, S], U8, name="xs", align_bytes=64)
         nc.vector.tensor_copy(xs[:], xs_table[:].indirect(offs_sb[:]))
         x_codes = []
@@ -114,7 +111,7 @@ def tile_picked_ybutter_none_po_kernel(tc, x_words, x_scales, w1, w2, own1, oth1
             x_codes.append(codes)
 
         y_banks = [psum.tile([P, S], F32, name="y_bank%d" % t, tag="bank%d" % t) for t in range(PACK)]
-        y0_late = psum.tile([P, S], F32, name="y0_late", tag="bank5")
+        y0_late = psum.tile([P, S], F32, name="y0_late", tag="bank4")
         groups = [(0, y_banks[0], slice(0, S // 2)), (0, y0_late, slice(S // 2, S))]
         groups.extend((t, y_banks[t], slice(0, S)) for t in range(1, PACK))
         for g in range(PASSES):
@@ -123,40 +120,40 @@ def tile_picked_ybutter_none_po_kernel(tc, x_words, x_scales, w1, w2, own1, oth1
                 nc.tensor.matmul_mx(
                     out=bank[:, tokens], lhsT=w1_codes[g][:, cols].bitcast(FP8X4), lhsT_scale=w1_scales[g][:, cols],
                     rhs=x_codes[g][:, tokens].bitcast(FP8X4), rhs_scale=xs[4 * g:, tokens], start=(g == 0), stop=(g == PASSES - 1))
-        for t, bank, tokens in groups:
-            nc.scalar.copy(out=y[t][:, tokens], in_=bank[:, tokens])
+        for i, (t, bank, tokens) in enumerate(groups):
+            copy = nc.vector.tensor_copy if i == 1 else nc.scalar.copy
+            copy(out=y[t][:, tokens], in_=bank[:, tokens])
 
-        partner, own_part = [], []
+        own_bank = psum.tile([P, CHUNKS, P], F32, name="own_bank", tag="bank7")
+        nc.tensor.transpose(own_bank[:, 0, :], own_rows[:], ident[:])
+        nc.scalar.activation(own_cols[:], own_bank[:, 0, 0:2 * CHUNKS], COPY)
+
+        partner = []
         for t in range(PACK):
             gathered = keep.tile([P, S], F32, name="partner1_%d" % t, tag="partner1_%d" % t)
             nc.vector.tensor_tensor(gathered[:], y[t][:].indirect(mix1_sb[:]), oth1_sb[:], MULT)
             partner.append(gathered)
-            if t < DIRECT:
-                product = keep.tile([P, S], F32, name="own1_direct%d" % t)
-                for tokens in [tokens for tile_t, bank, tokens in groups if tile_t == t]:
-                    nc.vector.tensor_tensor(product[:, tokens], y[t][:, tokens], own1_sb[:, tokens], MULT)
-                own_part.append(product[:])
-        rest = PACK - DIRECT
-        y_turned = [psum.tile([P, rest, P], F32, name="y_turned%d" % c, tag="bank%d" % (4 + c)) for c in range(CHUNKS)]
-        for e in range(rest):
+        turned_tags = [["bank5", "bank6"], ["bank7", "bank4"]]
+        y_turned = [[psum.tile([P, 2, 2, P], F32, name="y_turned%d_%d" % (u, b), tag=turned_tags[u][b]) for b in range(2)] for u in range(PAIRS)]
+        for u in range(PAIRS):
+            for e in range(2):
+                for c in range(CHUNKS):
+                    nc.tensor.transpose(y_turned[u][c // 2][:, c % 2, e, :], y[2 * u + e][:, c * P:(c + 1) * P], ident[:])
+        own_part = [psum.tile([P, S], F32, name="own1_back%d" % t, tag="bank%d" % t) for t in range(PACK)]
+        for u in range(PAIRS):
             for c in range(CHUNKS):
-                nc.tensor.transpose(y_turned[c][:, e, :], y[DIRECT + e][:, c * P:(c + 1) * P], ident[:])
-        back = [psum.tile([P, S], F32, name="own1_back%d" % e, tag="bank%d" % (DIRECT + e)) for e in range(rest)]
-        for c in range(CHUNKS):
-            scaled = keep.tile([P, rest, P], F32, name="scaled1_%d" % c, tag="scaled1_%d" % c, align_bytes=64)
-            nc.scalar.activation(scaled[:], y_turned[c][:], COPY, scale=own_cols[:, c:c + 1])
-            for e in range(rest):
-                nc.tensor.transpose(back[e][:, c * P:(c + 1) * P], scaled[:, e, :], ident[:])
-        own_part.extend(bank[:] for bank in back)
+                scaled = keep.tile([P, 2, P], F32, name="scaled1_%d_%d" % (u, c), tag="scaled1_%d_%d" % (u, c), align_bytes=64)
+                nc.scalar.activation(scaled[:], y_turned[u][c // 2][:, c % 2], COPY, scale=own_cols[:, c:c + 1])
+                for e in range(2):
+                    nc.tensor.transpose(own_part[2 * u + e][:, c * P:(c + 1) * P], scaled[:, e, :], ident[:])
         h1 = [keep.tile([P, S], F32, name="h1_%d" % t) for t in range(PACK)]
         for t in range(PACK):
-            nc.vector.tensor_tensor(h1[t][:], own_part[t], partner[t][:], ADD)
+            nc.vector.tensor_tensor(h1[t][:], own_part[t][:], partner[t][:], ADD)
 
-        w2_dealt = keep.tile([P, PACK * N], BF16, name="w2_dealt", tag="scaled1_2", align_bytes=64)
+        w2_dealt = keep.tile([P, PACK * N], BF16, name="w2_dealt", tag="scaled1_0_0", align_bytes=64)
         deal_and_round(nc.scalar.copy, w2_dealt, w2_raw, 0, P)
         w2_codes = keep.tile([P, N], U32, name="w2_codes", align_bytes=64)
         w2_scales = keep.tile([P, N], U8, name="w2_scales", align_bytes=64)
-        nc.vector.quantize_mx(out=w2_codes[:].bitcast(FP8X4), scales=w2_scales[:], in_=w2_dealt[:])
 
         h1_turned = [psum.tile([P, PACK, P], F32, name="h1_turned%d" % c, tag="bank%d" % (4 + c)) for c in range(CHUNKS)]
         own2_part = []
@@ -175,59 +172,59 @@ def tile_picked_ybutter_none_po_kernel(tc, x_words, x_scales, w1, w2, own1, oth1
         out_rows = out_0.rearrange("(p t) n -> p t n", t=PACK)
         words_hbm = out_1[0].rearrange("p n t -> p (n t)").bitcast(I32)
         partner2, h2_tiles, rounded_tiles = {}, {}, {}
+        last = CHUNKS - 1
 
-        def gather2(i):
-            lo, n = PIECES[i]
-            gathered = keep.tile([P, PACK, n], F32, name="partner2_%d" % i, tag="partner1_3" if i == 0 else "scaled1_3", align_bytes=None if i == 0 else 64)
+        def gather2(first, count):
+            lo, hi = first * P, (first + count) * P
+            gathered = keep.tile([P, PACK, hi - lo], F32, name="partner2_%d" % first, tag="partner1_%d" % (last - first))
             for t in range(PACK):
-                nc.vector.tensor_tensor(gathered[:, t, :], h1[t][:].indirect(mix2_sb[:, lo // 16:(lo + n) // 16]),
-                                        oth2_sb[:, lo:lo + n], MULT)
-            partner2[i] = gathered
+                nc.vector.tensor_tensor(gathered[:, t, :], h1[t][:].indirect(mix2_sb[:, lo // 16:hi // 16]), oth2_sb[:, lo:hi], MULT)
+            for c in range(count):
+                partner2[first + c] = gathered[:, :, c * P:(c + 1) * P]
 
-        def add2(i):
-            lo, n = PIECES[i]
-            h2 = ring.tile([P, n, PACK], BF16, name="h2", align_bytes=64)
-            own_view = own2_part[lo // P][:, :, lo % P:lo % P + n]
-            nc.vector.tensor_tensor(h2[:], own_view.rearrange("p t n -> p n t"), partner2[i][:].rearrange("p t n -> p n t"), ADD)
-            h2_tiles[i] = h2
+        def add2(c):
+            h2 = ring.tile([P, P, PACK], BF16, name="h2", align_bytes=64)
+            nc.vector.tensor_tensor(h2[:].rearrange("p (b i) t -> p b t i", i=PACK), own2_part[c][:].rearrange("p t (b i) -> p b t i", i=PACK),
+                                    partner2[c].rearrange("p t (b i) -> p b t i", i=PACK), ADD)
+            h2_tiles[c] = h2
 
-        def product2(i):
-            lo, n = PIECES[i]
-            codes = ring.tile([P, n], U32, name="h2_codes", align_bytes=64)
-            scales = ring.tile([P, n], U8, name="h2_scales", align_bytes=64)
-            nc.vector.quantize_mx(out=codes[:].bitcast(FP8X4), scales=scales[:], in_=h2_tiles[i][:].rearrange("p n t -> p (n t)"))
-            bank = psum.tile([P, PACK, n], F32, name="out_bank%d" % i, tag="bank%d" % (4 + i % CHUNKS))
+        def product2(c):
+            tokens = slice(c * P, (c + 1) * P)
+            codes = ring.tile([P, P], U32, name="h2_codes", align_bytes=64)
+            scales = ring.tile([P, P], U8, name="h2_scales", align_bytes=64)
+            nc.vector.quantize_mx(out=codes[:].bitcast(FP8X4), scales=scales[:], in_=h2_tiles[c][:].rearrange("p n t -> p (n t)"))
+            bank = psum.tile([P, PACK, P], F32, name="out_bank%d" % c, tag="bank%d" % (4 + c))
             for t in range(PACK):
                 cols = slice(t * P, (t + 1) * P)
                 nc.tensor.matmul_mx(out=bank[:, t, :], lhsT=w2_codes[:, cols].bitcast(FP8X4), lhsT_scale=w2_scales[:, cols],
                                     rhs=codes[:].bitcast(FP8X4), rhs_scale=scales[:], start=True, stop=True)
-            rounded = ring.tile([P, n, PACK], BF16, name="rounded", align_bytes=64)
-            result = keep.tile([P, PACK, n], F32, name="result%d" % i)
-            if i < len(PIECES) - 1:
+            rounded = ring.tile([P, P, PACK], BF16, name="rounded", align_bytes=64)
+            result = keep.tile([P, PACK, P], F32, name="result%d" % c)
+            if c < LATE:
                 nc.scalar.copy(out=rounded[:], in_=bank[:].rearrange("p t n -> p n t"))
             nc.scalar.copy(out=result[:], in_=bank[:])
-            nc.sync.dma_start(out=out_rows[:, :, lo:lo + n], in_=result[:])
-            if i == len(PIECES) - 1:
-                nc.vector.tensor_copy(out=rounded[:], in_=result[:].rearrange("p t n -> p n t"))
-            rounded_tiles[i] = rounded
+            nc.sync.dma_start(out=out_rows[:, :, tokens], in_=result[:])
+            if c >= LATE:
+                nc.vector.tensor_copy(out=rounded[:].rearrange("p (b i) t -> p b t i", i=PACK),
+                                      in_=result[:].rearrange("p t (b i) -> p b t i", i=PACK))
+            rounded_tiles[c] = rounded
 
-        def planes(i):
-            lo, n = PIECES[i]
-            nc.vector.quantize_mx(out=out_words[:, lo:lo + n].bitcast(FP8X4), scales=out_scales[:, lo:lo + n],
-                                  in_=rounded_tiles[i][:].rearrange("p n t -> p (n t)"))
-            nc.sync.dma_start(out=words_hbm[:, lo:lo + n], in_=out_words[:, lo:lo + n].bitcast(I32))
+        def planes(c):
+            tokens = slice(c * P, (c + 1) * P)
+            nc.vector.quantize_mx(out=out_words[:, tokens].bitcast(FP8X4), scales=out_scales[:, tokens],
+                                  in_=rounded_tiles[c][:].rearrange("p n t -> p (n t)"))
+            nc.sync.dma_start(out=words_hbm[:, tokens], in_=out_words[:, tokens].bitcast(I32))
 
-        last = len(PIECES) - 1
-        gather2(0)
-        gather2(1)
+        gather2(0, 2)
+        nc.vector.quantize_mx(out=w2_codes[:].bitcast(FP8X4), scales=w2_scales[:], in_=w2_dealt[:])
         add2(0)
-        for i in range(1, last + 1):
-            add2(i)
-            product2(i - 1)
-            if i > 1:
-                planes(i - 2)
-            if i < last:
-                gather2(i + 1)
+        for c in range(1, last + 1):
+            add2(c)
+            product2(c - 1)
+            if c > 1:
+                planes(c - 2)
+            if c < last:
+                gather2(c + 1, 1)
         product2(last)
         planes(last - 1)
         planes(last)

@@ -47,19 +47,20 @@ def tile_picked_ybutter_none_po_kernel(tc, x_words, x_scales, w1, w2, own1, oth1
         mix1_sb = lists.tile([P, S // 16], U16, name="mix1_sb")
         mix2_sb = lists.tile([P, S // 16], U16, name="mix2_sb")
 
-        w1_raw = [keep.tile([P, PACK, H], F32, name="w1_raw%d" % g) for g in range(PASSES)]
-        w2_raw = keep.tile([P, PACK, N], F32, name="w2_raw")
-        x_table = [keep.tile([P, T], I32, name="x_table%d" % g, align_bytes=64) for g in range(PASSES)]
-        xs_table = keep.tile([P, T], U8, name="xs_table", align_bytes=64)
-        oth1_sb = keep.tile([P, S], F32, name="oth1_sb")
-        oth2_sb = keep.tile([P, S], F32, name="oth2_sb")
+        w1_raw = [keep.tile([P, PACK, H], F32, name="w1_raw%d" % g, tag="w1_raw%d" % g, align_bytes=64) for g in range(PASSES)]
+        xs_table = keep.tile([P, T], U8, name="xs_table", tag="x_table0", align_bytes=64)
+        xs_picked = keep.tile([P, S], U8, name="xs_picked", align_bytes=64)
+        xs = [keep.tile([P, S], U8, name="xs%d" % g, align_bytes=64) for g in range(PASSES)]
         own_rows = keep.tile([P, P], F32, name="own_rows")
         own_cols = keep.tile([P, 2 * CHUNKS], F32, name="own_cols")
         ident = keep.tile([P, P], F32, name="ident")
         y = [keep.tile([P, S + SPARE], F32, name="y%d" % t, align_bytes=64) for t in range(PACK)]
 
-        nc.vector.memset(xs_table[:].bitcast(I32), 0)
+        nc.vector.memset(xs_table[32:64, :].bitcast(I32), 0)
+        nc.vector.memset(xs_table[64:P, :].bitcast(I32), 0)
         nc.gpsimd.memset(own_rows[:], 0.0)
+        for g in range(PASSES):
+            nc.gpsimd.memset(xs[g][:].bitcast(I32), 0)
         make_identity(nc, ident[:])
         for t in range(PACK):
             nc.gpsimd.memset(y[t][:, S:], 0.0)
@@ -68,42 +69,43 @@ def tile_picked_ybutter_none_po_kernel(tc, x_words, x_scales, w1, w2, own1, oth1
             nc.sync.dma_start(out=w1_raw[g][:], in_=w1[g * K_PASS:(g + 1) * K_PASS, :].rearrange("(p j) c -> p j c", j=PACK))
 
         def load_x(g):
-            nc.sync.dma_start(out=x_table[g][:], in_=x_words[g].rearrange("p n t -> p (n t)").bitcast(I32))
+            table = keep.tile([P, T], I32, name="x_table%d" % g, tag=("x_table0", "w1_raw0")[g], align_bytes=64)
+            nc.sync.dma_start(out=table[:], in_=x_words[g].rearrange("p n t -> p (n t)").bitcast(I32))
+            return table
 
-        def load_scales():
-            for q in range(4):
-                nc.sync.dma_start(out=xs_table[32 * q:32 * q + 4 * PASSES, :].bitcast(I32), in_=x_scales[:, 4 * q:4 * q + 4, :].bitcast(I32))
+        def place_scales(lo, hi):
+            for first in range(4 * lo, 4 * hi, 4):
+                g, q = first // 16, first // 4 % 4
+                nc.sync.dma_start(out=xs[g][32 * q:32 * q + 4, :].bitcast(I32), in_=xs_picked[first:first + 4, :].bitcast(I32))
 
-        load_w1(0)
+        nc.sync.dma_start(out=xs_table[0:32, :].bitcast(I32), in_=x_scales.rearrange("g q c -> (g q) c").bitcast(I32))
         nc.sync.dma_start(offs_sb[:], offs)
-        load_scales()
-        load_w1(1)
-        load_x(0)
-        load_x(1)
+        load_w1(0)
         nc.sync.dma_start(mix1_sb[:], mix1)
-        for r, own in enumerate((own1, own2)):
-            nc.sync.dma_start(out=own_rows[CHUNKS * r:CHUNKS * (r + 1), :], in_=own[0].rearrange("(c p) -> c p", p=P))
-        nc.sync.dma_start(out=oth1_sb[:], in_=oth1)
-        nc.sync.dma_start(out=w2_raw[:], in_=w2.rearrange("(p j) c -> p j c", j=PACK))
         nc.sync.dma_start(mix2_sb[:], mix2)
-        nc.sync.dma_start(out=oth2_sb[:], in_=oth2)
+        for r, own in enumerate((own1, own2)):
+            nc.scalar.dma_start(out=own_rows[CHUNKS * r:CHUNKS * (r + 1), :], in_=own[0].rearrange("(c p) -> c p", p=P))
+        load_w1(1)
+        nc.vector.tensor_copy(xs_picked[:], xs_table[:].indirect(offs_sb[:]))
+        place_scales(0, 6)
+        x_table = [load_x(0)]
+        place_scales(6, 8)
 
         w1_codes, w1_scales = [], []
         for g in range(PASSES):
             dealt = keep.tile([P, PACK * H], BF16, name="w1_dealt%d" % g, align_bytes=64)
             deal_and_round(nc.vector.tensor_copy, dealt, w1_raw[g], 0, V_SHARE)
             deal_and_round(nc.scalar.copy, dealt, w1_raw[g], V_SHARE, P)
-            codes = keep.tile([P, H], U32, name="w1_codes%d" % g, align_bytes=64)
+            codes = keep.tile([P, H], U32, name="w1_codes%d" % g, tag="w1_codes%d" % g, align_bytes=64)
             scales = keep.tile([P, H], U8, name="w1_scales%d" % g, align_bytes=64)
             nc.vector.quantize_mx(out=codes[:].bitcast(FP8X4), scales=scales[:], in_=dealt[:])
             w1_codes.append(codes)
             w1_scales.append(scales)
 
-        xs = keep.tile([P, S], U8, name="xs", align_bytes=64)
-        nc.vector.tensor_copy(xs[:], xs_table[:].indirect(offs_sb[:]))
+        x_table.append(load_x(1))
         x_codes = []
         for g in range(PASSES):
-            codes = keep.tile([P, S], U32, name="x_codes%d" % g, align_bytes=64)
+            codes = keep.tile([P, S], U32, name="x_codes%d" % g, tag="x_codes%d" % g, align_bytes=64)
             pieces = 2 if g == PASSES - 1 else 1
             for h in range(pieces):
                 lo, hi = h * S // pieces, (h + 1) * S // pieces
@@ -119,7 +121,13 @@ def tile_picked_ybutter_none_po_kernel(tc, x_words, x_scales, w1, w2, own1, oth1
                 cols = slice(t * P, (t + 1) * P)
                 nc.tensor.matmul_mx(
                     out=bank[:, tokens], lhsT=w1_codes[g][:, cols].bitcast(FP8X4), lhsT_scale=w1_scales[g][:, cols],
-                    rhs=x_codes[g][:, tokens].bitcast(FP8X4), rhs_scale=xs[4 * g:, tokens], start=(g == 0), stop=(g == PASSES - 1))
+                    rhs=x_codes[g][:, tokens].bitcast(FP8X4), rhs_scale=xs[g][:, tokens], start=(g == 0), stop=(g == PASSES - 1))
+        oth1_sb = keep.tile([P, S], F32, name="oth1_sb", tag="x_table0", align_bytes=64)
+        w2_raw = keep.tile([P, PACK, N], F32, name="w2_raw", tag="w1_codes0", align_bytes=64)
+        oth2_sb = keep.tile([P, S], F32, name="oth2_sb", tag="x_codes0", align_bytes=64)
+        nc.sync.dma_start(out=oth1_sb[:], in_=oth1)
+        nc.sync.dma_start(out=w2_raw[:], in_=w2.rearrange("(p j) c -> p j c", j=PACK))
+        nc.sync.dma_start(out=oth2_sb[:], in_=oth2)
         for i, (t, bank, tokens) in enumerate(groups):
             copy = nc.vector.tensor_copy if i == 1 else nc.scalar.copy
             copy(out=y[t][:, tokens], in_=bank[:, tokens])

@@ -56,9 +56,9 @@ def tile_picked_ybutter_none_po_kernel(tc, x_words, x_scales, w1, w2, own1, oth1
         ident = keep.tile([P, P], F32, name="ident")
         y = [keep.tile([P, S + SPARE], F32, name="y%d" % t, align_bytes=64) for t in range(PACK)]
 
+        nc.vector.memset(own_rows[:], 0.0)
         nc.vector.memset(xs_table[32:64, :].bitcast(I32), 0)
         nc.vector.memset(xs_table[64:P, :].bitcast(I32), 0)
-        nc.gpsimd.memset(own_rows[:], 0.0)
         for g in range(PASSES):
             nc.gpsimd.memset(xs[g][:].bitcast(I32), 0)
         make_identity(nc, ident[:])
@@ -84,7 +84,7 @@ def tile_picked_ybutter_none_po_kernel(tc, x_words, x_scales, w1, w2, own1, oth1
         nc.sync.dma_start(mix1_sb[:], mix1)
         nc.sync.dma_start(mix2_sb[:], mix2)
         for r, own in enumerate((own1, own2)):
-            nc.scalar.dma_start(out=own_rows[CHUNKS * r:CHUNKS * (r + 1), :], in_=own[0].rearrange("(c p) -> c p", p=P))
+            nc.sync.dma_start(out=own_rows[CHUNKS * r:CHUNKS * (r + 1), :], in_=own[0].rearrange("(c p) -> c p", p=P))
         load_w1(1)
         nc.vector.tensor_copy(xs_picked[:], xs_table[:].indirect(offs_sb[:]))
         place_scales(0, 6)
@@ -201,18 +201,27 @@ def tile_picked_ybutter_none_po_kernel(tc, x_words, x_scales, w1, w2, own1, oth1
             codes = ring.tile([P, P], U32, name="h2_codes", align_bytes=64)
             scales = ring.tile([P, P], U8, name="h2_scales", align_bytes=64)
             nc.vector.quantize_mx(out=codes[:].bitcast(FP8X4), scales=scales[:], in_=h2_tiles[c][:].rearrange("p n t -> p (n t)"))
-            bank = psum.tile([P, PACK, P], F32, name="out_bank%d" % c, tag="bank%d" % (4 + c))
-            for t in range(PACK):
-                cols = slice(t * P, (t + 1) * P)
-                nc.tensor.matmul_mx(out=bank[:, t, :], lhsT=w2_codes[:, cols].bitcast(FP8X4), lhsT_scale=w2_scales[:, cols],
-                                    rhs=codes[:].bitcast(FP8X4), rhs_scale=scales[:], start=True, stop=True)
+
+            def multiply(tag):
+                bank = psum.tile([P, PACK, P], F32, name="out_bank", tag=tag)
+                for t in range(PACK):
+                    cols = slice(t * P, (t + 1) * P)
+                    nc.tensor.matmul_mx(out=bank[:, t, :], lhsT=w2_codes[:, cols].bitcast(FP8X4), lhsT_scale=w2_scales[:, cols],
+                                        rhs=codes[:].bitcast(FP8X4), rhs_scale=scales[:], start=True, stop=True)
+                return bank
+
+            bank = multiply("bank%d" % (4 + c))
             rounded = ring.tile([P, P, PACK], BF16, name="rounded", align_bytes=64)
             result = keep.tile([P, PACK, P], F32, name="result%d" % c)
             if c < LATE:
                 nc.scalar.copy(out=rounded[:], in_=bank[:].rearrange("p t n -> p n t"))
+            if c == last:
+                nc.vector.tensor_copy(out=rounded[:], in_=bank[:].rearrange("p t n -> p n t"))
+                bank = multiply("bank0")
             nc.scalar.copy(out=result[:], in_=bank[:])
-            nc.sync.dma_start(out=out_rows[:, :, tokens], in_=result[:])
-            if c >= LATE:
+            store_queue = nc.scalar if c == last else nc.sync
+            store_queue.dma_start(out=out_rows[:, :, tokens], in_=result[:])
+            if LATE <= c < last:
                 nc.vector.tensor_copy(out=rounded[:].rearrange("p (b i) t -> p b t i", i=PACK),
                                       in_=result[:].rearrange("p t (b i) -> p b t i", i=PACK))
             rounded_tiles[c] = rounded
@@ -221,7 +230,9 @@ def tile_picked_ybutter_none_po_kernel(tc, x_words, x_scales, w1, w2, own1, oth1
             tokens = slice(c * P, (c + 1) * P)
             nc.vector.quantize_mx(out=out_words[:, tokens].bitcast(FP8X4), scales=out_scales[:, tokens],
                                   in_=rounded_tiles[c][:].rearrange("p n t -> p (n t)"))
-            nc.sync.dma_start(out=words_hbm[:, tokens], in_=out_words[:, tokens].bitcast(I32))
+            if c % 2 == 1:
+                pair = slice((c - 1) * P, (c + 1) * P)
+                nc.sync.dma_start(out=words_hbm[:, pair], in_=out_words[:, pair].bitcast(I32))
 
         gather2(0, 2)
         nc.vector.quantize_mx(out=w2_codes[:].bitcast(FP8X4), scales=w2_scales[:], in_=w2_dealt[:])

@@ -25,7 +25,7 @@ CHUNKS = S // P
 PAIRS = PACK // 2
 SPARE = 16
 V_SHARE = 80
-LATE = 2
+TURNED = (2, 3)
 
 
 def deal_and_round(engine_copy, dealt, raw, lo, hi):
@@ -40,7 +40,6 @@ def tile_picked_ybutter_none_po_kernel(tc, x_words, x_scales, w1, w2, own1, oth1
     with ExitStack() as ctx:
         lists = ctx.enter_context(tc.tile_pool(name="lists", bufs=1))
         keep = ctx.enter_context(tc.tile_pool(name="keep", bufs=1))
-        ring = ctx.enter_context(tc.tile_pool(name="ring", bufs=2))
         psum = ctx.enter_context(tc.psum_pool(name="psum", bufs=1))
 
         offs_sb = lists.tile([P, S // 16], U16, name="offs_sb")
@@ -52,7 +51,7 @@ def tile_picked_ybutter_none_po_kernel(tc, x_words, x_scales, w1, w2, own1, oth1
         xs_picked = keep.tile([P, S], U8, name="xs_picked", align_bytes=64)
         xs = [keep.tile([P, S], U8, name="xs%d" % g, align_bytes=64) for g in range(PASSES)]
         own_rows = keep.tile([P, P], F32, name="own_rows")
-        own_cols = keep.tile([P, 2 * CHUNKS], F32, name="own_cols")
+        own_cols = keep.tile([P, 3 * CHUNKS], F32, name="own_cols")
         ident = keep.tile([P, P], F32, name="ident")
         y = [keep.tile([P, S + SPARE], F32, name="y%d" % t, align_bytes=64) for t in range(PACK)]
 
@@ -83,13 +82,13 @@ def tile_picked_ybutter_none_po_kernel(tc, x_words, x_scales, w1, w2, own1, oth1
         load_w1(0)
         nc.sync.dma_start(mix1_sb[:], mix1)
         nc.sync.dma_start(mix2_sb[:], mix2)
-        for r, own in enumerate((own1, own2)):
+        for r, own in enumerate((own1, own2, oth2)):
             nc.sync.dma_start(out=own_rows[CHUNKS * r:CHUNKS * (r + 1), :], in_=own[0].rearrange("(c p) -> c p", p=P))
         load_w1(1)
         nc.vector.tensor_copy(xs_picked[:], xs_table[:].indirect(offs_sb[:]))
-        place_scales(0, 6)
+        place_scales(0, 5)
         x_table = [load_x(0)]
-        place_scales(6, 8)
+        place_scales(5, 8)
 
         w1_codes, w1_scales = [], []
         for g in range(PASSES):
@@ -124,17 +123,17 @@ def tile_picked_ybutter_none_po_kernel(tc, x_words, x_scales, w1, w2, own1, oth1
                     rhs=x_codes[g][:, tokens].bitcast(FP8X4), rhs_scale=xs[g][:, tokens], start=(g == 0), stop=(g == PASSES - 1))
         oth1_sb = keep.tile([P, S], F32, name="oth1_sb", tag="x_table0", align_bytes=64)
         w2_raw = keep.tile([P, PACK, N], F32, name="w2_raw", tag="w1_codes0", align_bytes=64)
-        oth2_sb = keep.tile([P, S], F32, name="oth2_sb", tag="x_codes0", align_bytes=64)
+        oth2_sb = keep.tile([P, S // 2], F32, name="oth2_sb", tag="x_codes0", align_bytes=64)
         nc.sync.dma_start(out=oth1_sb[:], in_=oth1)
         nc.sync.dma_start(out=w2_raw[:], in_=w2.rearrange("(p j) c -> p j c", j=PACK))
-        nc.sync.dma_start(out=oth2_sb[:], in_=oth2)
+        nc.sync.dma_start(out=oth2_sb[:], in_=oth2[:, 0:S // 2])
         for i, (t, bank, tokens) in enumerate(groups):
             copy = nc.vector.tensor_copy if i == 1 else nc.scalar.copy
             copy(out=y[t][:, tokens], in_=bank[:, tokens])
 
         own_bank = psum.tile([P, CHUNKS, P], F32, name="own_bank", tag="bank7")
         nc.tensor.transpose(own_bank[:, 0, :], own_rows[:], ident[:])
-        nc.scalar.activation(own_cols[:], own_bank[:, 0, 0:2 * CHUNKS], COPY)
+        nc.scalar.activation(own_cols[:], own_bank[:, 0, 0:3 * CHUNKS], COPY)
 
         partner = []
         for t in range(PACK):
@@ -163,90 +162,136 @@ def tile_picked_ybutter_none_po_kernel(tc, x_words, x_scales, w1, w2, own1, oth1
         w2_codes = keep.tile([P, N], U32, name="w2_codes", align_bytes=64)
         w2_scales = keep.tile([P, N], U8, name="w2_scales", align_bytes=64)
 
-        h1_turned = [psum.tile([P, PACK, P], F32, name="h1_turned%d" % c, tag="bank%d" % (4 + c)) for c in range(CHUNKS)]
-        own2_part = []
-        for c in range(CHUNKS):
-            for t in range(PACK):
-                nc.tensor.transpose(h1_turned[c][:, t, :], h1[t][:, c * P:(c + 1) * P], ident[:])
-            scaled = keep.tile([P, PACK, P], F32, name="scaled2_%d" % c)
-            nc.scalar.activation(scaled[:], h1_turned[c][:], COPY, scale=own_cols[:, CHUNKS + c:CHUNKS + c + 1])
-            back = psum.tile([P, PACK, P], F32, name="own2_back%d" % c, tag="bank%d" % c)
-            for t in range(PACK):
-                nc.tensor.transpose(back[:, t, :], scaled[:, t, :], ident[:])
-            own2_part.append(back)
-
         out_words = keep.tile([P, S], U32, name="out_words", align_bytes=64)
         out_scales = keep.tile([P, S], U8, name="out_scales", align_bytes=64)
         out_rows = out_0.rearrange("(p t) n -> p t n", t=PACK)
         words_hbm = out_1[0].rearrange("p n t -> p (n t)").bitcast(I32)
-        partner2, h2_tiles, rounded_tiles = {}, {}, {}
-        last = CHUNKS - 1
+        h1_turned = [psum.tile([P, PACK, P], F32, name="h1_turned%d" % c, tag="bank%d" % (4 + c)) for c in range(CHUNKS)]
+        partner_turned = {c: psum.tile([P, PACK, P], F32, name="partner_turned%d" % c, tag="bank%d" % c) for c in TURNED}
+        own2_part, partner2, h2_tiles, h2_back, h2_codes, results, rounded_tiles = {}, {}, {}, {}, {}, {}, {}
 
-        def gather2(first, count):
-            lo, hi = first * P, (first + count) * P
-            gathered = keep.tile([P, PACK, hi - lo], F32, name="partner2_%d" % first, tag="partner1_%d" % (last - first))
+        def turn_h1(c):
+            for t in range(PACK):
+                nc.tensor.transpose(h1_turned[c][:, t, :], h1[t][:, c * P:(c + 1) * P], ident[:])
+
+        def own_times2(c):
+            scale = own_cols[:, CHUNKS + c:CHUNKS + c + 1]
+            if c in TURNED:
+                scaled = keep.tile([P, P, PACK], F32, name="scaled2_%d" % c)
+                nc.scalar.activation(scaled[:], h1_turned[c][:].rearrange("p t f -> p f t"), COPY, scale=scale)
+                own2_part[c] = scaled
+            else:
+                scaled = keep.tile([P, PACK, P], F32, name="scaled2_%d" % c)
+                nc.scalar.activation(scaled[:], h1_turned[c][:], COPY, scale=scale)
+                back = psum.tile([P, PACK, P], F32, name="own2_back%d" % c, tag="bank%d" % c)
+                for t in range(PACK):
+                    nc.tensor.transpose(back[:, t, :], scaled[:, t, :], ident[:])
+                own2_part[c] = back
+
+        def gather2_plain(t):
+            lo, hi = TURNED[0] * P, (TURNED[-1] + 1) * P
+            gathered = keep.tile([P, hi - lo], F32, name="picked2_%d" % t)
+            nc.scalar.activation(gathered[:], h1[t][:].indirect(mix2_sb[:, lo // 16:hi // 16]), COPY)
+            for i, c in enumerate(TURNED):
+                nc.tensor.transpose(partner_turned[c][:, t, :], gathered[:, i * P:(i + 1) * P], ident[:])
+
+        def gather2(c):
+            lo, hi = c * P, (c + 1) * P
+            gathered = keep.tile([P, PACK, P], F32, name="partner2_%d" % c, tag="partner1_3")
             for t in range(PACK):
                 nc.vector.tensor_tensor(gathered[:, t, :], h1[t][:].indirect(mix2_sb[:, lo // 16:hi // 16]), oth2_sb[:, lo:hi], MULT)
-            for c in range(count):
-                partner2[first + c] = gathered[:, :, c * P:(c + 1) * P]
+            partner2[c] = gathered
 
         def add2(c):
-            h2 = ring.tile([P, P, PACK], BF16, name="h2", align_bytes=64)
+            h2 = keep.tile([P, P, PACK], BF16, name="h2_%d" % c, align_bytes=64)
             nc.vector.tensor_tensor(h2[:].rearrange("p (b i) t -> p b t i", i=PACK), own2_part[c][:].rearrange("p t (b i) -> p b t i", i=PACK),
-                                    partner2[c].rearrange("p t (b i) -> p b t i", i=PACK), ADD)
+                                    partner2[c][:].rearrange("p t (b i) -> p b t i", i=PACK), ADD)
             h2_tiles[c] = h2
 
+        def add2_turned(c):
+            turned = keep.tile([P, P, PACK], BF16, name="h2_turned%d" % c, align_bytes=64)
+            nc.vector.scalar_tensor_tensor(out=turned[:], in0=partner_turned[c][:].rearrange("p t f -> p f t"), scalar=own_cols[:, 2 * CHUNKS + c:2 * CHUNKS + c + 1],
+                                           in1=own2_part[c][:], op0=MULT, op1=ADD)
+            pairs = turned[:].rearrange("p f t -> p (f t)").bitcast(F32)
+            h2_back[c] = psum.tile([P, 2, P], F32, name="h2_back%d" % c, tag="bank%d" % c)
+            for e in range(2):
+                nc.tensor.transpose(h2_back[c][:, e, :], pairs[:, e:H // 2:2], ident[:])
+
+        def fetch_h2(c):
+            h2 = keep.tile([P, P, PACK], BF16, name="h2_%d" % c, align_bytes=64)
+            nc.scalar.copy(out=h2[:].rearrange("p n t -> p (n t)").bitcast(F32).rearrange("p (n e) -> p n e", e=2), in_=h2_back[c][:].rearrange("p e n -> p n e"))
+            h2_tiles[c] = h2
+
+        def multiply(c, number):
+            codes, scales = h2_codes[c]
+            bank = psum.tile([P, PACK, P], F32, name="out_bank", tag="bank%d" % number)
+            for t in range(PACK):
+                cols = slice(t * P, (t + 1) * P)
+                nc.tensor.matmul_mx(out=bank[:, t, :], lhsT=w2_codes[:, cols].bitcast(FP8X4), lhsT_scale=w2_scales[:, cols],
+                                    rhs=codes[:].bitcast(FP8X4), rhs_scale=scales[:], start=True, stop=True)
+            return bank
+
         def product2(c):
-            tokens = slice(c * P, (c + 1) * P)
-            codes = ring.tile([P, P], U32, name="h2_codes", align_bytes=64)
-            scales = ring.tile([P, P], U8, name="h2_scales", align_bytes=64)
+            codes = keep.tile([P, P], U32, name="h2_codes%d" % c, align_bytes=64)
+            scales = keep.tile([P, P], U8, name="h2_scales%d" % c, align_bytes=64)
             nc.vector.quantize_mx(out=codes[:].bitcast(FP8X4), scales=scales[:], in_=h2_tiles[c][:].rearrange("p n t -> p (n t)"))
+            h2_codes[c] = (codes, scales)
+            results[c] = (multiply(c, 4 + c), keep.tile([P, PACK, P], F32, name="result%d" % c))
 
-            def multiply(tag):
-                bank = psum.tile([P, PACK, P], F32, name="out_bank", tag=tag)
-                for t in range(PACK):
-                    cols = slice(t * P, (t + 1) * P)
-                    nc.tensor.matmul_mx(out=bank[:, t, :], lhsT=w2_codes[:, cols].bitcast(FP8X4), lhsT_scale=w2_scales[:, cols],
-                                        rhs=codes[:].bitcast(FP8X4), rhs_scale=scales[:], start=True, stop=True)
-                return bank
-
-            bank = multiply("bank%d" % (4 + c))
-            rounded = ring.tile([P, P, PACK], BF16, name="rounded", align_bytes=64)
-            result = keep.tile([P, PACK, P], F32, name="result%d" % c)
-            if c < LATE:
-                nc.scalar.copy(out=rounded[:], in_=bank[:].rearrange("p t n -> p n t"))
-            if c == last:
-                nc.vector.tensor_copy(out=rounded[:], in_=bank[:].rearrange("p t n -> p n t"))
-                bank = multiply("bank0")
+        def store_result(c, bank, queue):
+            result = results[c][1]
             nc.scalar.copy(out=result[:], in_=bank[:])
-            store_queue = nc.scalar if c == last else nc.sync
-            store_queue.dma_start(out=out_rows[:, :, tokens], in_=result[:])
-            if LATE <= c < last:
-                nc.vector.tensor_copy(out=rounded[:].rearrange("p (b i) t -> p b t i", i=PACK),
-                                      in_=result[:].rearrange("p t (b i) -> p b t i", i=PACK))
-            rounded_tiles[c] = rounded
+            queue.dma_start(out=out_rows[:, :, c * P:(c + 1) * P], in_=result[:])
+
+        def round_result(c, copy, source):
+            rounded_tiles[c] = keep.tile([P, P, PACK], BF16, name="rounded%d" % c, align_bytes=64)
+            copy(out=rounded_tiles[c][:], in_=source[:].rearrange("p t n -> p n t"))
 
         def planes(c):
             tokens = slice(c * P, (c + 1) * P)
             nc.vector.quantize_mx(out=out_words[:, tokens].bitcast(FP8X4), scales=out_scales[:, tokens],
                                   in_=rounded_tiles[c][:].rearrange("p n t -> p (n t)"))
-            if c % 2 == 1:
-                pair = slice((c - 1) * P, (c + 1) * P)
-                nc.sync.dma_start(out=words_hbm[:, pair], in_=out_words[:, pair].bitcast(I32))
 
-        gather2(0, 2)
+        def store_words(first):
+            pair = slice(first * P, (first + 2) * P)
+            nc.sync.dma_start(out=words_hbm[:, pair], in_=out_words[:, pair].bitcast(I32))
+
+        gather2_plain(0)
+        gather2_plain(1)
+        turn_h1(0)
+        own_times2(0)
+        gather2(0)
         nc.vector.quantize_mx(out=w2_codes[:].bitcast(FP8X4), scales=w2_scales[:], in_=w2_dealt[:])
+        gather2_plain(2)
+        gather2_plain(3)
         add2(0)
-        for c in range(1, last + 1):
-            add2(c)
-            product2(c - 1)
-            if c > 1:
-                planes(c - 2)
-            if c < last:
-                gather2(c + 1, 1)
-        product2(last)
-        planes(last - 1)
-        planes(last)
+        product2(0)
+        for c in (2, 3, 1):
+            turn_h1(c)
+            own_times2(c)
+        gather2(1)
+        add2_turned(2)
+        add2_turned(3)
+        store_result(0, results[0][0], nc.sync)
+        fetch_h2(2)
+        add2(1)
+        product2(2)
+        product2(1)
+        fetch_h2(3)
+        product2(3)
+        round_result(0, nc.vector.tensor_copy, results[0][1])
+        planes(0)
+        store_result(2, results[2][0], nc.sync)
+        round_result(2, nc.vector.tensor_copy, results[2][1])
+        planes(2)
+        store_result(1, results[1][0], nc.sync)
+        round_result(3, nc.vector.tensor_copy, results[3][0])
+        round_result(1, nc.vector.tensor_copy, results[1][1])
+        store_result(3, multiply(3, 0), nc.scalar)
+        planes(1)
+        store_words(0)
+        planes(3)
+        store_words(2)
         for q in range(4):
             queue = nc.sync if q % 2 == 0 else nc.scalar
             queue.dma_start(out=out_2[0, 4 * q:4 * q + 4, :].bitcast(I32), in_=out_scales[32 * q:32 * q + 4, :].bitcast(I32))

@@ -25,7 +25,8 @@ CHUNKS = S // P
 PAIRS = PACK // 2
 SPARE = 16
 V_SHARE = 80
-TURNED = (2, 3)
+TURNED = (2,)
+SHARED = 2
 
 
 def deal_and_round(engine_copy, dealt, raw, lo, hi):
@@ -40,13 +41,14 @@ def tile_picked_ybutter_none_po_kernel(tc, x_words, x_scales, w1, w2, own1, oth1
     with ExitStack() as ctx:
         lists = ctx.enter_context(tc.tile_pool(name="lists", bufs=1))
         keep = ctx.enter_context(tc.tile_pool(name="keep", bufs=1))
+        early = ctx.enter_context(tc.tile_pool(name="early", bufs=1))
         psum = ctx.enter_context(tc.psum_pool(name="psum", bufs=1))
 
         offs_sb = lists.tile([P, S // 16], U16, name="offs_sb")
         mix1_sb = lists.tile([P, S // 16], U16, name="mix1_sb")
         mix2_sb = lists.tile([P, S // 16], U16, name="mix2_sb")
 
-        w1_raw = [keep.tile([P, PACK, H], F32, name="w1_raw%d" % g, tag="w1_raw%d" % g, align_bytes=64) for g in range(PASSES)]
+        w1_raw = [keep.tile([P, PACK, H], F32, name="w1_raw0", tag="w1_raw0", align_bytes=64), early.tile([P, PACK, H], F32, name="w1_raw1", offset=0)]
         xs_table = keep.tile([P, T], U8, name="xs_table", tag="x_table0", align_bytes=64)
         xs_picked = keep.tile([P, S], U8, name="xs_picked", align_bytes=64)
         xs = [keep.tile([P, S], U8, name="xs%d" % g, align_bytes=64) for g in range(PASSES)]
@@ -121,12 +123,24 @@ def tile_picked_ybutter_none_po_kernel(tc, x_words, x_scales, w1, w2, own1, oth1
                 nc.tensor.matmul_mx(
                     out=bank[:, tokens], lhsT=w1_codes[g][:, cols].bitcast(FP8X4), lhsT_scale=w1_scales[g][:, cols],
                     rhs=x_codes[g][:, tokens].bitcast(FP8X4), rhs_scale=xs[g][:, tokens], start=(g == 0), stop=(g == PASSES - 1))
-        oth1_sb = keep.tile([P, S], F32, name="oth1_sb", tag="x_table0", align_bytes=64)
-        w2_raw = keep.tile([P, PACK, N], F32, name="w2_raw", tag="w1_codes0", align_bytes=64)
-        oth2_sb = keep.tile([P, S // 2], F32, name="oth2_sb", tag="x_codes0", align_bytes=64)
+        w2_raw = [early.tile([P, PACK, N // 2], F32, name="w2_raw0", offset=0),
+                  keep.tile([P, PACK, N // 2], F32, name="w2_raw1", tag="w1_codes1", align_bytes=64)]
+        oth1_sb = early.tile([P, S], F32, name="oth1_sb", offset=PACK * N * 2)
+        oth2_sb = keep.tile([P, 2 * P], F32, name="oth2_sb", tag="x_codes0", align_bytes=64)
+        oth2_last = keep.tile([P, P], F32, name="oth2_last", tag="x_codes1", align_bytes=64)
+        w2_rows = w2.rearrange("(p j) c -> p j c", j=PACK)
+        nc.sync.dma_start(out=w2_raw[0][:], in_=w2_rows[:, :, 0:N // 2])
         nc.sync.dma_start(out=oth1_sb[:], in_=oth1)
-        nc.sync.dma_start(out=w2_raw[:], in_=w2.rearrange("(p j) c -> p j c", j=PACK))
-        nc.sync.dma_start(out=oth2_sb[:], in_=oth2[:, 0:S // 2])
+        nc.sync.dma_start(out=w2_raw[1][:], in_=w2_rows[:, :, N // 2:N])
+        w2_dealt = keep.tile([P, PACK * N], BF16, name="w2_dealt", tag="w2_dealt", align_bytes=64)
+
+        def round_w2(half, copy, lo, hi):
+            copy(out=w2_dealt[:].rearrange("p (t m j) -> p m j t", t=PACK, j=PACK)[:, half * P // 2 + lo:half * P // 2 + hi],
+                 in_=w2_raw[half][:].rearrange("p j (m t) -> p m j t", t=PACK)[:, lo:hi])
+
+        round_w2(0, nc.vector.tensor_copy, 0, P // 2)
+        nc.sync.dma_start(out=oth2_sb[:], in_=oth2[:, 0:2 * P])
+        nc.sync.dma_start(out=oth2_last[:], in_=oth2[:, 3 * P:4 * P])
         for i, (t, bank, tokens) in enumerate(groups):
             copy = nc.vector.tensor_copy if i == 1 else nc.scalar.copy
             copy(out=y[t][:, tokens], in_=bank[:, tokens])
@@ -137,9 +151,10 @@ def tile_picked_ybutter_none_po_kernel(tc, x_words, x_scales, w1, w2, own1, oth1
 
         partner = []
         for t in range(PACK):
-            gathered = keep.tile([P, S], F32, name="partner1_%d" % t, tag="partner1_%d" % t)
-            nc.vector.tensor_tensor(gathered[:], y[t][:].indirect(mix1_sb[:]), oth1_sb[:], MULT)
-            partner.append(gathered)
+            if t == 0:
+                partner.append(early.tile([P, S], F32, name="partner1_0", offset=0))
+            else:
+                partner.append(keep.tile([P, S], F32, name="partner1_%d" % t, tag="partner1_%d" % (0 if t == 3 else t)))
         turned_tags = [["bank5", "bank6"], ["bank7", "bank4"]]
         y_turned = [[psum.tile([P, 2, 2, P], F32, name="y_turned%d_%d" % (u, b), tag=turned_tags[u][b]) for b in range(2)] for u in range(PAIRS)]
         for u in range(PAIRS):
@@ -154,11 +169,22 @@ def tile_picked_ybutter_none_po_kernel(tc, x_words, x_scales, w1, w2, own1, oth1
                 for e in range(2):
                     nc.tensor.transpose(own_part[2 * u + e][:, c * P:(c + 1) * P], scaled[:, e, :], ident[:])
         h1 = [keep.tile([P, S], F32, name="h1_%d" % t) for t in range(PACK)]
-        for t in range(PACK):
+
+        def gather1(t):
+            nc.vector.tensor_tensor(partner[t][:], y[t][:].indirect(mix1_sb[:]), oth1_sb[:], MULT)
+
+        def add1(t):
             nc.vector.tensor_tensor(h1[t][:], own_part[t][:], partner[t][:], ADD)
 
-        w2_dealt = keep.tile([P, PACK * N], BF16, name="w2_dealt", tag="scaled1_0_0", align_bytes=64)
-        deal_and_round(nc.scalar.copy, w2_dealt, w2_raw, 0, P)
+        for t in range(PACK):
+            gather1(t)
+        for t in range(PACK - 1):
+            add1(t)
+        own_last = keep.tile([P, S], F32, name="own_last")
+        nc.scalar.copy(out=own_last[:], in_=own_part[PACK - 1][:])
+        nc.gpsimd.tensor_tensor(h1[PACK - 1][:], own_last[:], partner[PACK - 1][:], ADD)
+        round_w2(1, nc.scalar.copy, 0, P // 4)
+        round_w2(1, nc.scalar.copy, P // 4, P // 2)
         w2_codes = keep.tile([P, N], U32, name="w2_codes", align_bytes=64)
         w2_scales = keep.tile([P, N], U8, name="w2_scales", align_bytes=64)
 
@@ -181,31 +207,33 @@ def tile_picked_ybutter_none_po_kernel(tc, x_words, x_scales, w1, w2, own1, oth1
                 nc.scalar.activation(scaled[:], h1_turned[c][:].rearrange("p t f -> p f t"), COPY, scale=scale)
                 own2_part[c] = scaled
             else:
-                scaled = keep.tile([P, PACK, P], F32, name="scaled2_%d" % c)
+                scaled = keep.tile([P, PACK, P], F32, name="scaled2_%d" % c, tag="scaled2_%d" % c)
                 nc.scalar.activation(scaled[:], h1_turned[c][:], COPY, scale=scale)
                 back = psum.tile([P, PACK, P], F32, name="own2_back%d" % c, tag="bank%d" % c)
                 for t in range(PACK):
                     nc.tensor.transpose(back[:, t, :], scaled[:, t, :], ident[:])
                 own2_part[c] = back
 
-        def gather2_plain(t):
-            lo, hi = TURNED[0] * P, (TURNED[-1] + 1) * P
-            gathered = keep.tile([P, hi - lo], F32, name="picked2_%d" % t)
-            nc.scalar.activation(gathered[:], h1[t][:].indirect(mix2_sb[:, lo // 16:hi // 16]), COPY)
-            for i, c in enumerate(TURNED):
-                nc.tensor.transpose(partner_turned[c][:, t, :], gathered[:, i * P:(i + 1) * P], ident[:])
+        def gather2_plain(t, gathered, count):
+            c = TURNED[0]
+            nc.scalar.activation(gathered, h1[t][:].indirect(mix2_sb[:, c * P // 16:(c + count) * P // 16]), COPY)
+            nc.tensor.transpose(partner_turned[c][:, t, :], gathered[:, 0:P], ident[:])
 
-        def gather2(c):
-            lo, hi = c * P, (c + 1) * P
-            gathered = keep.tile([P, PACK, P], F32, name="partner2_%d" % c, tag="partner1_3")
+        def gather2(first, count, tag):
+            lo, hi = first * P, (first + count) * P
+            gathered = keep.tile([P, PACK, hi - lo], F32, name="partner2_%d" % first, tag=tag)
             for t in range(PACK):
                 nc.vector.tensor_tensor(gathered[:, t, :], h1[t][:].indirect(mix2_sb[:, lo // 16:hi // 16]), oth2_sb[:, lo:hi], MULT)
-            partner2[c] = gathered
+            for c in range(count):
+                partner2[first + c] = gathered[:, :, c * P:(c + 1) * P]
 
         def add2(c):
-            h2 = keep.tile([P, P, PACK], BF16, name="h2_%d" % c, align_bytes=64)
-            nc.vector.tensor_tensor(h2[:].rearrange("p (b i) t -> p b t i", i=PACK), own2_part[c][:].rearrange("p t (b i) -> p b t i", i=PACK),
-                                    partner2[c][:].rearrange("p t (b i) -> p b t i", i=PACK), ADD)
+            if c == 1:
+                h2 = joint[:, SHARED * P:].bitcast(BF16).rearrange("p (n t) -> p n t", t=PACK)
+            else:
+                h2 = keep.tile([P, P, PACK], BF16, name="h2_%d" % c, align_bytes=64)[:]
+            nc.vector.tensor_tensor(h2.rearrange("p (b i) t -> p b t i", i=PACK), own2_part[c][:].rearrange("p t (b i) -> p b t i", i=PACK),
+                                    partner2[c].rearrange("p t (b i) -> p b t i", i=PACK), ADD)
             h2_tiles[c] = h2
 
         def add2_turned(c):
@@ -220,7 +248,7 @@ def tile_picked_ybutter_none_po_kernel(tc, x_words, x_scales, w1, w2, own1, oth1
         def fetch_h2(c):
             h2 = keep.tile([P, P, PACK], BF16, name="h2_%d" % c, align_bytes=64)
             nc.scalar.copy(out=h2[:].rearrange("p n t -> p (n t)").bitcast(F32).rearrange("p (n e) -> p n e", e=2), in_=h2_back[c][:].rearrange("p e n -> p n e"))
-            h2_tiles[c] = h2
+            h2_tiles[c] = h2[:]
 
         def multiply(c, number):
             codes, scales = h2_codes[c]
@@ -234,7 +262,7 @@ def tile_picked_ybutter_none_po_kernel(tc, x_words, x_scales, w1, w2, own1, oth1
         def product2(c):
             codes = keep.tile([P, P], U32, name="h2_codes%d" % c, align_bytes=64)
             scales = keep.tile([P, P], U8, name="h2_scales%d" % c, align_bytes=64)
-            nc.vector.quantize_mx(out=codes[:].bitcast(FP8X4), scales=scales[:], in_=h2_tiles[c][:].rearrange("p n t -> p (n t)"))
+            nc.vector.quantize_mx(out=codes[:].bitcast(FP8X4), scales=scales[:], in_=h2_tiles[c].rearrange("p n t -> p (n t)"))
             h2_codes[c] = (codes, scales)
             results[c] = (multiply(c, 4 + c), keep.tile([P, PACK, P], F32, name="result%d" % c))
 
@@ -256,40 +284,47 @@ def tile_picked_ybutter_none_po_kernel(tc, x_words, x_scales, w1, w2, own1, oth1
             pair = slice(first * P, (first + 2) * P)
             nc.sync.dma_start(out=words_hbm[:, pair], in_=out_words[:, pair].bitcast(I32))
 
-        gather2_plain(0)
-        gather2_plain(1)
-        turn_h1(0)
-        own_times2(0)
-        gather2(0)
-        nc.vector.quantize_mx(out=w2_codes[:].bitcast(FP8X4), scales=w2_scales[:], in_=w2_dealt[:])
-        gather2_plain(2)
-        gather2_plain(3)
-        add2(0)
-        product2(0)
-        for c in (2, 3, 1):
+        def finish(c):
+            store_result(c, results[c][0], nc.sync)
+            round_result(c, nc.scalar.copy, results[c][0])
+
+        joint = keep.tile([P, PACK * P], F32, name="joint", tag="x_codes0", align_bytes=64)
+        last_partner = joint[:].rearrange("p (t n) -> p t n", t=PACK)
+        wide_picked = keep.tile([P, SHARED, 2 * P], F32, name="wide_picked", tag="scaled1_1_3", align_bytes=64)
+        for t in range(SHARED):
+            gather2_plain(t, wide_picked[:, t, :], 2)
+        picked = keep.tile([P, PACK - SHARED, P], F32, name="picked", tag="scaled1_1_2", align_bytes=64)
+        for t in range(SHARED, PACK):
+            gather2_plain(t, picked[:, t - SHARED, :], 1)
+        for c in (0, 2, 1, 3):
             turn_h1(c)
             own_times2(c)
-        gather2(1)
+        gather2(0, 2, "partner1_2")
+        nc.vector.quantize_mx(out=w2_codes[:].bitcast(FP8X4), scales=w2_scales[:], in_=w2_dealt[:])
+        nc.gpsimd.tensor_tensor(last_partner[:, 0:SHARED, :], wide_picked[:, :, P:2 * P], oth2_last[:].unsqueeze(1).to_broadcast([P, SHARED, P]), MULT)
+        add2(0)
         add2_turned(2)
-        add2_turned(3)
-        store_result(0, results[0][0], nc.sync)
-        fetch_h2(2)
+        product2(0)
         add2(1)
-        product2(2)
+        fetch_h2(2)
         product2(1)
-        fetch_h2(3)
+        product2(2)
+        for t in range(SHARED, PACK):
+            nc.vector.tensor_tensor(last_partner[:, t, :], h1[t][:].indirect(mix2_sb[:, 3 * P // 16:4 * P // 16]), oth2_last[:], MULT)
+        partner2[3] = last_partner
+        finish(0)
+        add2(3)
         product2(3)
-        round_result(0, nc.vector.tensor_copy, results[0][1])
-        planes(0)
-        store_result(2, results[2][0], nc.sync)
-        round_result(2, nc.vector.tensor_copy, results[2][1])
-        planes(2)
         store_result(1, results[1][0], nc.sync)
+        store_result(2, results[2][0], nc.sync)
+        round_result(1, nc.scalar.copy, results[1][0])
+        planes(0)
+        round_result(2, nc.vector.tensor_copy, results[2][1])
         round_result(3, nc.vector.tensor_copy, results[3][0])
-        round_result(1, nc.vector.tensor_copy, results[1][1])
         store_result(3, multiply(3, 0), nc.scalar)
         planes(1)
         store_words(0)
+        planes(2)
         planes(3)
         store_words(2)
         for q in range(4):

@@ -126,7 +126,8 @@ def tile_picked_ybutter_none_po_kernel(tc, x_words, x_scales, w1, w2, own1, oth1
         w2_raw = [early.tile([P, PACK, N // 2], F32, name="w2_raw0", offset=0),
                   keep.tile([P, PACK, N // 2], F32, name="w2_raw1", tag="w1_codes1", align_bytes=64)]
         oth1_sb = early.tile([P, S], F32, name="oth1_sb", offset=PACK * N * 2)
-        oth2_sb = keep.tile([P, 2 * P], F32, name="oth2_sb", tag="x_codes0", align_bytes=64)
+        joint = keep.tile([P, (PACK + 1) * P], F32, name="joint", tag="x_codes0", align_bytes=64)
+        oth2_sb = joint[:, 0:2 * P]
         oth2_last = keep.tile([P, P], F32, name="oth2_last", tag="x_codes1", align_bytes=64)
         w2_rows = w2.rearrange("(p j) c -> p j c", j=PACK)
         nc.sync.dma_start(out=w2_raw[0][:], in_=w2_rows[:, :, 0:N // 2])
@@ -139,7 +140,7 @@ def tile_picked_ybutter_none_po_kernel(tc, x_words, x_scales, w1, w2, own1, oth1
                  in_=w2_raw[half][:].rearrange("p j (m t) -> p m j t", t=PACK)[:, lo:hi])
 
         round_w2(0, nc.vector.tensor_copy, 0, P // 2)
-        nc.sync.dma_start(out=oth2_sb[:], in_=oth2[:, 0:2 * P])
+        nc.sync.dma_start(out=oth2_sb, in_=oth2[:, 0:2 * P])
         nc.sync.dma_start(out=oth2_last[:], in_=oth2[:, 3 * P:4 * P])
         for i, (t, bank, tokens) in enumerate(groups):
             copy = nc.vector.tensor_copy if i == 1 else nc.scalar.copy
@@ -229,7 +230,7 @@ def tile_picked_ybutter_none_po_kernel(tc, x_words, x_scales, w1, w2, own1, oth1
 
         def add2(c):
             if c == 1:
-                h2 = joint[:, SHARED * P:].bitcast(BF16).rearrange("p (n t) -> p n t", t=PACK)
+                h2 = joint[:, (PACK - 1) * P:].bitcast(BF16).rearrange("p (n t) -> p n t", t=PACK)
             else:
                 h2 = keep.tile([P, P, PACK], BF16, name="h2_%d" % c, align_bytes=64)[:]
             nc.vector.tensor_tensor(h2.rearrange("p (b i) t -> p b t i", i=PACK), own2_part[c][:].rearrange("p t (b i) -> p b t i", i=PACK),
@@ -288,8 +289,7 @@ def tile_picked_ybutter_none_po_kernel(tc, x_words, x_scales, w1, w2, own1, oth1
             store_result(c, results[c][0], nc.sync)
             round_result(c, nc.scalar.copy, results[c][0])
 
-        joint = keep.tile([P, PACK * P], F32, name="joint", tag="x_codes0", align_bytes=64)
-        last_partner = joint[:].rearrange("p (t n) -> p t n", t=PACK)
+        last_partner = joint[:, 0:PACK * P].rearrange("p (t n) -> p t n", t=PACK)
         wide_picked = keep.tile([P, SHARED, 2 * P], F32, name="wide_picked", tag="scaled1_1_3", align_bytes=64)
         for t in range(SHARED):
             gather2_plain(t, wide_picked[:, t, :], 2)
@@ -301,6 +301,11 @@ def tile_picked_ybutter_none_po_kernel(tc, x_words, x_scales, w1, w2, own1, oth1
             own_times2(c)
         gather2(0, 2, "partner1_2")
         nc.vector.quantize_mx(out=w2_codes[:].bitcast(FP8X4), scales=w2_scales[:], in_=w2_dealt[:])
+
+        def gather2_last(t):
+            nc.vector.tensor_tensor(last_partner[:, t, :], h1[t][:].indirect(mix2_sb[:, 3 * P // 16:4 * P // 16]), oth2_last[:], MULT)
+
+        gather2_last(2)
         nc.gpsimd.tensor_tensor(last_partner[:, 0:SHARED, :], wide_picked[:, :, P:2 * P], oth2_last[:].unsqueeze(1).to_broadcast([P, SHARED, P]), MULT)
         add2(0)
         add2_turned(2)
@@ -309,22 +314,21 @@ def tile_picked_ybutter_none_po_kernel(tc, x_words, x_scales, w1, w2, own1, oth1
         fetch_h2(2)
         product2(1)
         product2(2)
-        for t in range(SHARED, PACK):
-            nc.vector.tensor_tensor(last_partner[:, t, :], h1[t][:].indirect(mix2_sb[:, 3 * P // 16:4 * P // 16]), oth2_last[:], MULT)
+        gather2_last(3)
         partner2[3] = last_partner
         finish(0)
         add2(3)
         product2(3)
         store_result(1, results[1][0], nc.sync)
         store_result(2, results[2][0], nc.sync)
-        round_result(1, nc.scalar.copy, results[1][0])
         planes(0)
+        round_result(1, nc.vector.tensor_copy, results[1][1])
         round_result(2, nc.vector.tensor_copy, results[2][1])
-        round_result(3, nc.vector.tensor_copy, results[3][0])
-        store_result(3, multiply(3, 0), nc.scalar)
+        store_result(3, results[3][0], nc.scalar)
         planes(1)
         store_words(0)
         planes(2)
+        round_result(3, nc.vector.tensor_copy, multiply(3, 0))
         planes(3)
         store_words(2)
         for q in range(4):

@@ -70,7 +70,7 @@ def tile_picked_ybutter_none_po_kernel(tc, x_words, x_scales, w1, w2, own1, oth1
             nc.sync.dma_start(out=w1_raw[g][:], in_=w1[g * K_PASS:(g + 1) * K_PASS, :].rearrange("(p j) c -> p j c", j=PACK))
 
         def load_x(g):
-            table = keep.tile([P, T], I32, name="x_table%d" % g, tag=("x_table0", "w1_raw0")[g], align_bytes=64)
+            table = keep.tile([P, T], I32, name="x_table%d" % g, tag=("x_table1", "x_table0")[g], align_bytes=64)
             nc.sync.dma_start(out=table[:], in_=x_words[g].rearrange("p n t -> p (n t)").bitcast(I32))
             return table
 
@@ -87,9 +87,10 @@ def tile_picked_ybutter_none_po_kernel(tc, x_words, x_scales, w1, w2, own1, oth1
         for r, own in enumerate((own1, own2, oth2)):
             nc.sync.dma_start(out=own_rows[CHUNKS * r:CHUNKS * (r + 1), :], in_=own[0].rearrange("(c p) -> c p", p=P))
         load_w1(1)
+        x_table = [load_x(0)]
         nc.vector.tensor_copy(xs_picked[:], xs_table[:].indirect(offs_sb[:]))
         place_scales(0, 5)
-        x_table = [load_x(0)]
+        x_table.append(load_x(1))
         place_scales(5, 8)
 
         w1_codes, w1_scales = [], []
@@ -103,7 +104,6 @@ def tile_picked_ybutter_none_po_kernel(tc, x_words, x_scales, w1, w2, own1, oth1
             w1_codes.append(codes)
             w1_scales.append(scales)
 
-        x_table.append(load_x(1))
         x_codes = []
         for g in range(PASSES):
             codes = keep.tile([P, S], U32, name="x_codes%d" % g, tag="x_codes%d" % g, align_bytes=64)

@@ -26,7 +26,7 @@ PAIRS = PACK // 2
 SPARE = 16
 V_SHARE = 80
 TURNED = (2,)
-SHARED = 2
+SHARED = 3
 
 
 def deal_and_round(engine_copy, dealt, raw, lo, hi):
@@ -305,7 +305,6 @@ def tile_picked_ybutter_none_po_kernel(tc, x_words, x_scales, w1, w2, own1, oth1
         def gather2_last(t):
             nc.vector.tensor_tensor(last_partner[:, t, :], h1[t][:].indirect(mix2_sb[:, 3 * P // 16:4 * P // 16]), oth2_last[:], MULT)
 
-        gather2_last(2)
         nc.gpsimd.tensor_tensor(last_partner[:, 0:SHARED, :], wide_picked[:, :, P:2 * P], oth2_last[:].unsqueeze(1).to_broadcast([P, SHARED, P]), MULT)
         add2(0)
         add2_turned(2)

from contextlib import ExitStack

import concourse.mybir as mybir
from concourse.masks import make_identity

K, T, S, H, N = 1024, 2048, 512, 512, 512
FLOPS = 2 * S * H * (K + N)

F32 = mybir.dt.float32
BF16 = mybir.dt.bfloat16
I32 = mybir.dt.int32
U32 = mybir.dt.uint32
U16 = mybir.dt.uint16
U8 = mybir.dt.uint8
FP8X4 = mybir.dt.float8_e4m3fn_x4
MULT = mybir.AluOpType.mult
ADD = mybir.AluOpType.add
COPY = mybir.ActivationFunctionType.Copy

P = 128
PACK = 4
K_PASS = P * PACK
PASSES = K // K_PASS
CHUNKS = S // P
PAIRS = PACK // 2
SPARE = 16
V_SHARE = 80
TURNED = (2,)
SHARED = 3


def deal_and_round(engine_copy, dealt, raw, lo, hi):
    engine_copy(
        out=dealt[:].rearrange("p (t m j) -> p m t j", t=PACK, j=PACK)[:, lo:hi],
        in_=raw[:].rearrange("p j (m t) -> p m t j", t=PACK)[:, lo:hi],
    )


def tile_picked_ybutter_none_po_kernel(tc, x_words, x_scales, w1, w2, own1, oth1, own2, oth2, offs, mix1, mix2, out_0, out_1, out_2):
    nc = tc.nc
    with ExitStack() as ctx:
        lists = ctx.enter_context(tc.tile_pool(name="lists", bufs=1))
        keep = ctx.enter_context(tc.tile_pool(name="keep", bufs=1))
        early = ctx.enter_context(tc.tile_pool(name="early", bufs=1))
        psum = ctx.enter_context(tc.psum_pool(name="psum", bufs=1))

        offs_sb = lists.tile([P, S // 16], U16, name="offs_sb")
        mix1_sb = lists.tile([P, S // 16], U16, name="mix1_sb")
        mix2_sb = lists.tile([P, S // 16], U16, name="mix2_sb")

        w1_raw = [keep.tile([P, PACK, H], F32, name="w1_raw0", tag="w1_raw0", align_bytes=64), early.tile([P, PACK, H], F32, name="w1_raw1", offset=0)]
        xs_table = keep.tile([P, T], U8, name="xs_table", tag="x_table0", align_bytes=64)
        xs_picked = keep.tile([P, S], U8, name="xs_picked", align_bytes=64)
        xs = [keep.tile([P, S], U8, name="xs%d" % g, align_bytes=64) for g in range(PASSES)]
        own_rows = keep.tile([P, P], F32, name="own_rows")
        own_cols = keep.tile([P, 3 * CHUNKS], F32, name="own_cols")
        ident = keep.tile([P, P], F32, name="ident")
        y = [keep.tile([P, S + SPARE], F32, name="y%d" % t, align_bytes=64) for t in range(PACK)]

        nc.vector.memset(own_rows[:], 0.0)
        nc.vector.memset(xs_table[32:64, :].bitcast(I32), 0)
        nc.vector.memset(xs_table[64:P, :].bitcast(I32), 0)
        for g in range(PASSES):
            nc.gpsimd.memset(xs[g][:].bitcast(I32), 0)
        make_identity(nc, ident[:])
        for t in range(PACK):
            nc.gpsimd.memset(y[t][:, S:], 0.0)

        def load_w1(g):
            nc.sync.dma_start(out=w1_raw[g][:], in_=w1[g * K_PASS:(g + 1) * K_PASS, :].rearrange("(p j) c -> p j c", j=PACK))

        def load_x(g):
            table = keep.tile([P, T], I32, name="x_table%d" % g, tag=("x_table1", "x_table0")[g], align_bytes=64)
            nc.sync.dma_start(out=table[:], in_=x_words[g].rearrange("p n t -> p (n t)").bitcast(I32))
            return table

        def place_scales(lo, hi):
            for first in range(4 * lo, 4 * hi, 4):
                g, q = first // 16, first // 4 % 4
                nc.sync.dma_start(out=xs[g][32 * q:32 * q + 4, :].bitcast(I32), in_=xs_picked[first:first + 4, :].bitcast(I32))

        nc.sync.dma_start(out=xs_table[0:32, :].bitcast(I32), in_=x_scales.rearrange("g q c -> (g q) c").bitcast(I32))
        nc.sync.dma_start(offs_sb[:], offs)
        load_w1(0)
        nc.sync.dma_start(mix1_sb[:], mix1)
        nc.sync.dma_start(mix2_sb[:], mix2)
        for r, own in enumerate((own1, own2, oth2)):
            nc.sync.dma_start(out=own_rows[CHUNKS * r:CHUNKS * (r + 1), :], in_=own[0].rearrange("(c p) -> c p", p=P))
        load_w1(1)
        x_table = [load_x(0)]
        nc.vector.tensor_copy(xs_picked[:], xs_table[:].indirect(offs_sb[:]))
        place_scales(0, 5)
        x_table.append(load_x(1))
        place_scales(5, 8)

        w1_codes, w1_scales = [], []
        for g in range(PASSES):
            dealt = keep.tile([P, PACK * H], BF16, name="w1_dealt%d" % g, align_bytes=64)
            deal_and_round(nc.vector.tensor_copy, dealt, w1_raw[g], 0, V_SHARE)
            deal_and_round(nc.scalar.copy, dealt, w1_raw[g], V_SHARE, P)
            codes = keep.tile([P, H], U32, name="w1_codes%d" % g, tag="w1_codes%d" % g, align_bytes=64)
            scales = keep.tile([P, H], U8, name="w1_scales%d" % g, align_bytes=64)
            nc.vector.quantize_mx(out=codes[:].bitcast(FP8X4), scales=scales[:], in_=dealt[:])
            w1_codes.append(codes)
            w1_scales.append(scales)

        x_codes = []
        for g in range(PASSES):
            codes = keep.tile([P, S], U32, name="x_codes%d" % g, tag="x_codes%d" % g, align_bytes=64)
            pieces = 2 if g == PASSES - 1 else 1
            for h in range(pieces):
                lo, hi = h * S // pieces, (h + 1) * S // pieces
                nc.vector.tensor_copy(codes[:, lo:hi], x_table[g][:].bitcast(U32).indirect(offs_sb[:, lo // 16:hi // 16]))
            x_codes.append(codes)

        y_banks = [psum.tile([P, S], F32, name="y_bank%d" % t, tag="bank%d" % t) for t in range(PACK)]
        y0_late = psum.tile([P, S], F32, name="y0_late", tag="bank4")
        groups = [(0, y_banks[0], slice(0, S // 2)), (0, y0_late, slice(S // 2, S))]
        groups.extend((t, y_banks[t], slice(0, S)) for t in range(1, PACK))
        for g in range(PASSES):
            for t, bank, tokens in groups:
                cols = slice(t * P, (t + 1) * P)
                nc.tensor.matmul_mx(
                    out=bank[:, tokens], lhsT=w1_codes[g][:, cols].bitcast(FP8X4), lhsT_scale=w1_scales[g][:, cols],
                    rhs=x_codes[g][:, tokens].bitcast(FP8X4), rhs_scale=xs[g][:, tokens], start=(g == 0), stop=(g == PASSES - 1))
        w2_raw = [early.tile([P, PACK, N // 2], F32, name="w2_raw0", offset=0),
                  keep.tile([P, PACK, N // 2], F32, name="w2_raw1", tag="w1_codes1", align_bytes=64)]
        oth1_sb = early.tile([P, S], F32, name="oth1_sb", offset=PACK * N * 2)
        joint = keep.tile([P, (PACK + 1) * P], F32, name="joint", tag="x_codes0", align_bytes=64)
        oth2_sb = joint[:, 0:2 * P]
        oth2_last = keep.tile([P, P], F32, name="oth2_last", tag="x_codes1", align_bytes=64)
        w2_rows = w2.rearrange("(p j) c -> p j c", j=PACK)
        nc.sync.dma_start(out=w2_raw[0][:], in_=w2_rows[:, :, 0:N // 2])
        nc.sync.dma_start(out=oth1_sb[:], in_=oth1)
        nc.sync.dma_start(out=w2_raw[1][:], in_=w2_rows[:, :, N // 2:N])
        w2_dealt = keep.tile([P, PACK * N], BF16, name="w2_dealt", tag="w2_dealt", align_bytes=64)

        def round_w2(half, copy, lo, hi):
            copy(out=w2_dealt[:].rearrange("p (t m j) -> p m j t", t=PACK, j=PACK)[:, half * P // 2 + lo:half * P // 2 + hi],
                 in_=w2_raw[half][:].rearrange("p j (m t) -> p m j t", t=PACK)[:, lo:hi])

        round_w2(0, nc.vector.tensor_copy, 0, P // 2)
        nc.sync.dma_start(out=oth2_sb, in_=oth2[:, 0:2 * P])
        nc.sync.dma_start(out=oth2_last[:], in_=oth2[:, 3 * P:4 * P])
        for i, (t, bank, tokens) in enumerate(groups):
            copy = nc.vector.tensor_copy if i == 1 else nc.scalar.copy
            copy(out=y[t][:, tokens], in_=bank[:, tokens])

        own_bank = psum.tile([P, CHUNKS, P], F32, name="own_bank", tag="bank7")
        nc.tensor.transpose(own_bank[:, 0, :], own_rows[:], ident[:])
        nc.scalar.activation(own_cols[:], own_bank[:, 0, 0:3 * CHUNKS], COPY)

        partner = []
        for t in range(PACK):
            if t == 0:
                partner.append(early.tile([P, S], F32, name="partner1_0", offset=0))
            else:
                partner.append(keep.tile([P, S], F32, name="partner1_%d" % t, tag="partner1_%d" % (0 if t == 3 else t)))
        turned_tags = [["bank5", "bank6"], ["bank7", "bank4"]]
        y_turned = [[psum.tile([P, 2, 2, P], F32, name="y_turned%d_%d" % (u, b), tag=turned_tags[u][b]) for b in range(2)] for u in range(PAIRS)]
        for u in range(PAIRS):
            for e in range(2):
                for c in range(CHUNKS):
                    nc.tensor.transpose(y_turned[u][c // 2][:, c % 2, e, :], y[2 * u + e][:, c * P:(c + 1) * P], ident[:])
        own_part = [psum.tile([P, S], F32, name="own1_back%d" % t, tag="bank%d" % t) for t in range(PACK)]
        for u in range(PAIRS):
            for c in range(CHUNKS):
                scaled = keep.tile([P, 2, P], F32, name="scaled1_%d_%d" % (u, c), tag="scaled1_%d_%d" % (u, c), align_bytes=64)
                nc.scalar.activation(scaled[:], y_turned[u][c // 2][:, c % 2], COPY, scale=own_cols[:, c:c + 1])
                for e in range(2):
                    nc.tensor.transpose(own_part[2 * u + e][:, c * P:(c + 1) * P], scaled[:, e, :], ident[:])
        h1 = [keep.tile([P, S], F32, name="h1_%d" % t) for t in range(PACK)]

        def gather1(t):
            nc.vector.tensor_tensor(partner[t][:], y[t][:].indirect(mix1_sb[:]), oth1_sb[:], MULT)

        def add1(t):
            nc.vector.tensor_tensor(h1[t][:], own_part[t][:], partner[t][:], ADD)

        for t in range(PACK):
            gather1(t)
        for t in range(PACK - 1):
            add1(t)
        own_last = keep.tile([P, S], F32, name="own_last")
        nc.scalar.copy(out=own_last[:], in_=own_part[PACK - 1][:])
        nc.gpsimd.tensor_tensor(h1[PACK - 1][:], own_last[:], partner[PACK - 1][:], ADD)
        round_w2(1, nc.scalar.copy, 0, P // 4)
        round_w2(1, nc.scalar.copy, P // 4, P // 2)
        w2_codes = keep.tile([P, N], U32, name="w2_codes", align_bytes=64)
        w2_scales = keep.tile([P, N], U8, name="w2_scales", align_bytes=64)

        out_words = keep.tile([P, S], U32, name="out_words", align_bytes=64)
        out_scales = keep.tile([P, S], U8, name="out_scales", align_bytes=64)
        out_rows = out_0.rearrange("(p t) n -> p t n", t=PACK)
        words_hbm = out_1[0].rearrange("p n t -> p (n t)").bitcast(I32)
        h1_turned = [psum.tile([P, PACK, P], F32, name="h1_turned%d" % c, tag="bank%d" % (4 + c)) for c in range(CHUNKS)]
        partner_turned = {c: psum.tile([P, PACK, P], F32, name="partner_turned%d" % c, tag="bank%d" % c) for c in TURNED}
        own2_part, partner2, h2_tiles, h2_back, h2_codes, results, rounded_tiles = {}, {}, {}, {}, {}, {}, {}

        def turn_h1(c):
            for t in range(PACK):
                nc.tensor.transpose(h1_turned[c][:, t, :], h1[t][:, c * P:(c + 1) * P], ident[:])

        def own_times2(c):
            scale = own_cols[:, CHUNKS + c:CHUNKS + c + 1]
            if c in TURNED:
                scaled = keep.tile([P, P, PACK], F32, name="scaled2_%d" % c)
                nc.scalar.activation(scaled[:], h1_turned[c][:].rearrange("p t f -> p f t"), COPY, scale=scale)
                own2_part[c] = scaled
            else:
                scaled = keep.tile([P, PACK, P], F32, name="scaled2_%d" % c, tag="scaled2_%d" % c)
                nc.scalar.activation(scaled[:], h1_turned[c][:], COPY, scale=scale)
                back = psum.tile([P, PACK, P], F32, name="own2_back%d" % c, tag="bank%d" % c)
                for t in range(PACK):
                    nc.tensor.transpose(back[:, t, :], scaled[:, t, :], ident[:])
                own2_part[c] = back

        def gather2_plain(t, gathered, count):
            c = TURNED[0]
            nc.scalar.activation(gathered, h1[t][:].indirect(mix2_sb[:, c * P // 16:(c + count) * P // 16]), COPY)
            nc.tensor.transpose(partner_turned[c][:, t, :], gathered[:, 0:P], ident[:])

        def gather2(first, count, tag):
            lo, hi = first * P, (first + count) * P
            gathered = keep.tile([P, PACK, hi - lo], F32, name="partner2_%d" % first, tag=tag)
            for t in range(PACK):
                nc.vector.tensor_tensor(gathered[:, t, :], h1[t][:].indirect(mix2_sb[:, lo // 16:hi // 16]), oth2_sb[:, lo:hi], MULT)
            for c in range(count):
                partner2[first + c] = gathered[:, :, c * P:(c + 1) * P]

        def add2(c):
            if c == 1:
                h2 = joint[:, (PACK - 1) * P:].bitcast(BF16).rearrange("p (n t) -> p n t", t=PACK)
            else:
                h2 = keep.tile([P, P, PACK], BF16, name="h2_%d" % c, align_bytes=64)[:]
            nc.vector.tensor_tensor(h2.rearrange("p (b i) t -> p b t i", i=PACK), own2_part[c][:].rearrange("p t (b i) -> p b t i", i=PACK),
                                    partner2[c].rearrange("p t (b i) -> p b t i", i=PACK), ADD)
            h2_tiles[c] = h2

        def add2_turned(c):
            turned = keep.tile([P, P, PACK], BF16, name="h2_turned%d" % c, align_bytes=64)
            nc.vector.scalar_tensor_tensor(out=turned[:], in0=partner_turned[c][:].rearrange("p t f -> p f t"), scalar=own_cols[:, 2 * CHUNKS + c:2 * CHUNKS + c + 1],
                                           in1=own2_part[c][:], op0=MULT, op1=ADD)
            pairs = turned[:].rearrange("p f t -> p (f t)").bitcast(F32)
            h2_back[c] = psum.tile([P, 2, P], F32, name="h2_back%d" % c, tag="bank%d" % c)
            for e in range(2):
                nc.tensor.transpose(h2_back[c][:, e, :], pairs[:, e:H // 2:2], ident[:])

        def fetch_h2(c):
            h2 = keep.tile([P, P, PACK], BF16, name="h2_%d" % c, align_bytes=64)
            nc.scalar.copy(out=h2[:].rearrange("p n t -> p (n t)").bitcast(F32).rearrange("p (n e) -> p n e", e=2), in_=h2_back[c][:].rearrange("p e n -> p n e"))
            h2_tiles[c] = h2[:]

        def multiply(c, number):
            codes, scales = h2_codes[c]
            bank = psum.tile([P, PACK, P], F32, name="out_bank", tag="bank%d" % number)
            for t in range(PACK):
                cols = slice(t * P, (t + 1) * P)
                nc.tensor.matmul_mx(out=bank[:, t, :], lhsT=w2_codes[:, cols].bitcast(FP8X4), lhsT_scale=w2_scales[:, cols],
                                    rhs=codes[:].bitcast(FP8X4), rhs_scale=scales[:], start=True, stop=True)
            return bank

        def product2(c):
            codes = keep.tile([P, P], U32, name="h2_codes%d" % c, align_bytes=64)
            scales = keep.tile([P, P], U8, name="h2_scales%d" % c, align_bytes=64)
            nc.vector.quantize_mx(out=codes[:].bitcast(FP8X4), scales=scales[:], in_=h2_tiles[c].rearrange("p n t -> p (n t)"))
            h2_codes[c] = (codes, scales)
            results[c] = (multiply(c, 4 + c), keep.tile([P, PACK, P], F32, name="result%d" % c))

        def store_result(c, bank, queue):
            result = results[c][1]
            nc.scalar.copy(out=result[:], in_=bank[:])
            queue.dma_start(out=out_rows[:, :, c * P:(c + 1) * P], in_=result[:])

        def round_result(c, copy, source):
            rounded_tiles[c] = keep.tile([P, P, PACK], BF16, name="rounded%d" % c, align_bytes=64)
            copy(out=rounded_tiles[c][:], in_=source[:].rearrange("p t n -> p n t"))

        def planes(c):
            tokens = slice(c * P, (c + 1) * P)
            nc.vector.quantize_mx(out=out_words[:, tokens].bitcast(FP8X4), scales=out_scales[:, tokens],
                                  in_=rounded_tiles[c][:].rearrange("p n t -> p (n t)"))

        def store_words(first):
            pair = slice(first * P, (first + 2) * P)
            nc.sync.dma_start(out=words_hbm[:, pair], in_=out_words[:, pair].bitcast(I32))

        def finish(c):
            store_result(c, results[c][0], nc.sync)
            round_result(c, nc.scalar.copy, results[c][0])

        last_partner = joint[:, 0:PACK * P].rearrange("p (t n) -> p t n", t=PACK)
        wide_picked = keep.tile([P, SHARED, 2 * P], F32, name="wide_picked", tag="scaled1_1_3", align_bytes=64)
        for t in range(SHARED):
            gather2_plain(t, wide_picked[:, t, :], 2)
        picked = keep.tile([P, PACK - SHARED, P], F32, name="picked", tag="scaled1_1_2", align_bytes=64)
        for t in range(SHARED, PACK):
            gather2_plain(t, picked[:, t - SHARED, :], 1)
        for c in (0, 2, 1, 3):
            turn_h1(c)
            own_times2(c)
        gather2(0, 2, "partner1_2")
        nc.vector.quantize_mx(out=w2_codes[:].bitcast(FP8X4), scales=w2_scales[:], in_=w2_dealt[:])

        def gather2_last(t):
            nc.vector.tensor_tensor(last_partner[:, t, :], h1[t][:].indirect(mix2_sb[:, 3 * P // 16:4 * P // 16]), oth2_last[:], MULT)

        nc.gpsimd.tensor_tensor(last_partner[:, 0:SHARED, :], wide_picked[:, :, P:2 * P], oth2_last[:].unsqueeze(1).to_broadcast([P, SHARED, P]), MULT)
        add2(0)
        add2_turned(2)
        product2(0)
        add2(1)
        fetch_h2(2)
        product2(1)
        product2(2)
        gather2_last(3)
        partner2[3] = last_partner
        finish(0)
        add2(3)
        product2(3)
        store_result(1, results[1][0], nc.sync)
        store_result(2, results[2][0], nc.sync)
        planes(0)
        round_result(1, nc.vector.tensor_copy, results[1][1])
        round_result(2, nc.vector.tensor_copy, results[2][1])
        store_result(3, results[3][0], nc.scalar)
        planes(1)
        store_words(0)
        planes(2)
        round_result(3, nc.vector.tensor_copy, multiply(3, 0))
        planes(3)
        store_words(2)
        for q in range(4):
            queue = nc.sync if q % 2 == 0 else nc.scalar
            queue.dma_start(out=out_2[0, 4 * q:4 * q + 4, :].bitcast(I32), in_=out_scales[32 * q:32 * q + 4, :].bitcast(I32))
